import numpy as np
import ml_dtypes


def mxq(x, axis, fmt="e4m3"):
    dtype, down = {"e4m3": (ml_dtypes.float8_e4m3fn, 7), "e5m2": (ml_dtypes.float8_e5m2, 14)}[fmt]
    v = np.moveaxis(np.asarray(x, np.float32).astype(ml_dtypes.bfloat16).astype(np.float64), axis, -1)
    blocks = v.reshape(v.shape[:-1] + (-1, 32))
    amax = np.abs(blocks).max(-1, keepdims=True)
    byte = np.maximum(np.where(amax > 0, np.frexp(amax)[1] - 1 + 127, 0) - down, 1)
    scale = np.exp2(byte - 127.0)
    codes = (blocks / scale).astype(np.float32).astype(dtype).astype(np.float64)
    return np.moveaxis((codes * scale).reshape(v.shape), -1, axis)


WIDE = False


def mx_kscale(k):
    if not WIDE:
        return np.ones(k)
    levels = np.array([10, -10, 5, -5, 0])
    if k % 512:
        return np.exp2(np.random.permutation(np.resize(levels, k // 32))).repeat(32)
    a = np.empty((k // 512, 16))
    for p in range(k // 512):
        a[p, :8] = np.random.permutation(np.resize(levels, 8))
        for g in range(8):
            far = levels[np.abs(levels - a[p, g]) >= 10]
            a[p, g + 8] = far[np.random.randint(len(far))]
    return np.exp2(a.ravel()).repeat(32)


def f64(x):
    return np.asarray(x).astype(np.float64)


def striped(idx):
    return np.tile(idx.reshape(-1, 16).T, (8, 1)).astype(np.uint16)


def unstriped(offs):
    return offs[:16].T.reshape(-1).astype(np.int64)


E2M1 = np.array([0.0, 0.5, 1.0, 1.5, 2.0, 3.0, 4.0, 6.0, -0.0, -0.5, -1.0, -1.5, -2.0, -3.0, -4.0, -6.0])


def pack_weight(w, fmt):
    k, n = w.shape
    w = f64(np.asarray(w, np.float32).astype(ml_dtypes.bfloat16)).reshape(k // 32, 32, n)
    amax = np.abs(w).max(1)
    if fmt == "e4m3":
        byte = np.frexp(amax)[1] - 1 + 127 - 7
    else:
        mant, ex = np.frexp(amax / 6.0)
        byte = np.where(mant > 0.5, ex, ex - 1) + 127
    byte = np.clip(np.where(amax > 0, byte, 1), 1, 254)
    scaled = (w * np.exp2(127.0 - byte)[:, None, :]).reshape(k, n).astype(np.float32)
    by_word = np.ascontiguousarray(scaled.reshape(k // 512, 128, 4, n).transpose(0, 1, 3, 2))
    if fmt == "e4m3":
        words = by_word.astype(ml_dtypes.float8_e4m3fn).view(np.uint8)
    else:
        c = by_word.astype(ml_dtypes.float4_e2m1fn).view(np.uint8) & 0xF
        words = (c[..., 0::2] | (c[..., 1::2] << 4)).reshape(k // 512, 128, 2 * n)
    return np.ascontiguousarray(words), np.ascontiguousarray(byte.astype(np.uint8).reshape(k // 512, 16, n))


def unpack_weight(words, scales, fmt):
    g, _, n = scales.shape
    words = np.ascontiguousarray(words).reshape(g, 128, n, -1)
    if fmt == "e4m3":
        vals = words.view(ml_dtypes.float8_e4m3fn).astype(np.float64)
    else:
        nib = np.empty((g, 128, n, 4), np.uint8)
        nib[..., 0::2] = words & 0xF
        nib[..., 1::2] = words >> 4
        vals = E2M1[nib]
    vals = vals * np.repeat(np.exp2(scales.astype(np.float64) - 127.0), 8, axis=1)[..., None]
    return vals.transpose(0, 1, 3, 2).reshape(g * 512, n)


K, T, E1, C1, E2, C2, H = 1536, 1024, 8, 128, 4, 256, 512
N = 128


def deal(E, C):
    slot_token = np.random.permutation(T)
    return slot_token, None, np.random.uniform(0.2, 1.0, T)


def by_expert(wq, xq, E, C):
    return np.concatenate([wq[e].T @ xq[:, e * C:(e + 1) * C] for e in range(E)], axis=1)


def setup_inputs():
    n = np.random.standard_normal
    s = mx_kscale(K)
    u = mx_kscale(H)
    slots1, pos1, g1 = deal(E1, C1)
    slots2, pos2, g2 = deal(E2, C2)
    x = pack_weight(n((K, T)) * s[:, None], "e4m3")
    w1 = [pack_weight(m, "e2m1") for m in n((E1, K, H)) / np.sqrt(K) / s[None, :, None] * u]
    w2 = [pack_weight(m, "e2m1") for m in n((E2, H, N)) / np.sqrt(H) / u[None, :, None]]
    return {
        "x_words": x[0],
        "x_scales": x[1],
        "w1_words": np.stack([m[0] for m in w1]),
        "w1_scales": np.stack([m[1] for m in w1]),
        "w2_words": np.stack([m[0] for m in w2]),
        "w2_scales": np.stack([m[1] for m in w2]),
        "gate1": (np.tile(g1, (128, 1))).astype(np.float32),
        "gate2": (np.tile(g2, (128, 1))).astype(np.float32),
        "offs": striped(slots1),
        "offs2": striped(slots2),
    }


def reference(x_words, x_scales, w1_words, w1_scales, w2_words, w2_scales, gate1, gate2, offs, offs2):
    w1 = np.stack([unpack_weight(w1_words[e], w1_scales[e], "e2m1") for e in range(E1)])
    w2 = np.stack([unpack_weight(w2_words[e], w2_scales[e], "e2m1") for e in range(E2)])
    idx, idx2 = unstriped(offs), unstriped(offs2)
    xq = unpack_weight(x_words, x_scales, "e4m3")[:, idx]
    h = by_expert(w1, xq, E1, C1)
    c = np.zeros((H, T))
    c[:, idx] = f64(gate1[:1]) * h
    y = by_expert(w2, mxq(c[:, idx2], 0, "e4m3"), E2, C2)
    out = np.zeros((N, T))
    out[:, idx2] = f64(gate2[:1]) * y
    return out

@@ -1,0 +1,193 @@
+from contextlib import ExitStack
+
+import concourse.mybir as mybir
+from concourse.masks import make_identity
+
+K, T, E1, C1, E2, C2, H, N = 1536, 1024, 8, 128, 4, 256, 512, 128
+FLOPS = 2 * T * K * H + 2 * T * H * N
+
+F32 = mybir.dt.float32
+BF16 = mybir.dt.bfloat16
+I32 = mybir.dt.int32
+U32 = mybir.dt.uint32
+U16 = mybir.dt.uint16
+U8 = mybir.dt.uint8
+FP8X4 = mybir.dt.float8_e4m3fn_x4
+FP4X4 = mybir.dt.float4_e2m1fn_x4
+COPY = mybir.ActivationFunctionType.Copy
+MULT = mybir.AluOpType.mult
+
+P = 128
+PASSES = K // 512
+PAIRS = E1 // 2
+PAIR_SLOTS = 2 * C1
+HALF = T // 2
+PAIR_PLANES = 2 * PASSES
+
+
+def tile_moe_ser_none_kernel(
+    tc, x_words, x_scales, w1_words, w1_scales, w2_words, w2_scales, gate1, gate2, offs, offs2, out
+):
+    nc = tc.nc
+    with ExitStack() as ctx:
+        lists = ctx.enter_context(tc.tile_pool(name="lists", bufs=1))
+        keep = ctx.enter_context(tc.tile_pool(name="keep", bufs=1))
+        ring = ctx.enter_context(tc.tile_pool(name="ring", bufs=2))
+        psum = ctx.enter_context(tc.psum_pool(name="psum", bufs=2))
+
+        list1 = lists.tile([P, T // 16], U16, name="list1")
+        list2 = lists.tile([P, T // 16], U16, name="list2")
+        nc.sync.dma_start(list1[:], offs)
+
+        xs = keep.tile([P, T], U8, name="xs", tag="odd", align_bytes=64)
+        nc.gpsimd.memset(xs[:].bitcast(I32), 0)
+        for s in range(PASSES):
+            nc.scalar.dma_start(xs[s:64:4, :].bitcast(I32), x_scales[s].bitcast(I32))
+
+        grow = keep.tile([P, P], F32, name="grow")
+        nc.gpsimd.memset(grow[:], 0.0)
+        nc.scalar.dma_start(grow[0:E1, :], gate1[0].rearrange("(e c) -> e c", e=E1))
+
+        xw = []
+        for s in range(PASSES):
+            t = keep.tile([P, T], I32, name="xw%d" % s, tag="xw%d" % s)
+            nc.sync.dma_start(t[:], x_words[s].rearrange("p t d -> p (t d)").bitcast(I32))
+            xw.append(t)
+
+        ws = keep.tile([P, 2 * PAIR_PLANES * H], U8, name="ws", align_bytes=64)
+        nc.vector.memset(ws[:].bitcast(I32), 0)
+        xp = keep.tile([P, 4 * T], U8, name="xp", align_bytes=64)
+        nc.vector.memset(xp[:].bitcast(I32), 0)
+
+        def load_w1_scales(queue, first_pair, pairs):
+            src = w1_scales[2 * first_pair : 2 * (first_pair + pairs)].rearrange("e s (q r) i -> r q (e s) i", r=4)
+            c0 = (first_pair % 2) * PAIR_PLANES * H
+            for r in range(4):
+                dst = ws[r:P:32, c0 : c0 + pairs * PAIR_PLANES * H].bitcast(I32)
+                queue.dma_start(dst.rearrange("q (g i) -> q g i", i=H // 4), src[r].bitcast(I32))
+
+        def load_w1_words(pair):
+            t = keep.tile([P, PAIR_PLANES, 2 * H], U8, name="w1_%d" % pair, tag=("even", "odd")[pair % 2], align_bytes=64)
+            src = w1_words[2 * pair : 2 * pair + 2].rearrange("e s p b -> p (e s) b")
+            nc.sync.dma_start(t[:].bitcast(I32), src.bitcast(I32))
+            return t
+
+        w1 = [load_w1_words(0)]
+        load_w1_scales(nc.scalar, 0, 2)
+
+        ident = keep.tile([P, P], F32, name="ident")
+        make_identity(nc, ident[:])
+        nc.sync.dma_start(list2[:], offs2)
+        gps = psum.tile([P, P], F32, name="gps", tag="y")
+        nc.tensor.transpose(gps[:], grow[:], ident[:])
+        gcol = keep.tile([P, E1], F32, name="gcol")
+        nc.scalar.activation(gcol[:], gps[:, 0:E1], COPY)
+
+        xsg = keep.tile([P, T], U8, name="xsg", align_bytes=64)
+        for half in range(2):
+            cols = list1[:, half * HALF // 16 : (half + 1) * HALF // 16]
+            nc.vector.tensor_copy(xsg[:, half * HALF : (half + 1) * HALF], xs[:].indirect(cols))
+        for q in range(4):
+            dst = xp[32 * q : 32 * q + 4, :].bitcast(I32).rearrange("r (s t) -> r s t", s=4)
+            nc.scalar.dma_start(dst, xsg[16 * q : 16 * q + 16, :].bitcast(I32))
+        w1.append(load_w1_words(1))
+
+        xg = {}
+        for half in range(2):
+            cols = list1[:, half * HALF // 16 : (half + 1) * HALF // 16]
+            for s in range(PASSES):
+                t = keep.tile([P, HALF], U32, name="xg%d_%d" % (half, s), align_bytes=64)
+                nc.vector.tensor_copy(t[:], xw[s][:].bitcast(U32).indirect(cols))
+                xg[(half, s)] = t
+
+        g2 = keep.tile([P, T], F32, name="g2", tag="xw0")
+        nc.sync.dma_start(g2[:], gate2)
+
+        cw = [keep.tile([P, T], F32, name="cw%d" % u) for u in range(2)]
+        for pair in range(PAIRS):
+            tr = psum.tile([P, 2, PAIR_SLOTS], F32, name="tr", tag="tr")
+            for j in range(2):
+                e = 2 * pair + j
+                half, col = divmod(e * C1, HALF)
+                h = psum.tile([P, H], F32, name="h", tag="h", bufs=4)
+                for s in range(PASSES):
+                    g = j * PASSES + s
+                    c0 = ((pair % 2) * PAIR_PLANES + g) * H
+                    nc.tensor.matmul_mx(
+                        out=h[:],
+                        lhsT=xg[(half, s)][:, col : col + C1].bitcast(FP8X4),
+                        lhsT_scale=xp[:, s * T + e * C1 : s * T + (e + 1) * C1],
+                        rhs=w1[pair][:, g, :].bitcast(FP4X4),
+                        rhs_scale=ws[:, c0 : c0 + H],
+                        start=(s == 0),
+                        stop=(s == PASSES - 1),
+                    )
+                hb = ring.tile([P, H], BF16, name="hb", bufs=4)
+                nc.scalar.activation(
+                    hb[:].rearrange("c (u p v) -> c u p v", u=2, v=2),
+                    h[:].rearrange("c (p u v) -> c u p v", u=2, v=2),
+                    COPY,
+                    scale=gcol[:, e : e + 1],
+                )
+                for u in range(2):
+                    nc.tensor.transpose(tr[:, u, j * C1 : (j + 1) * C1], hb[:].bitcast(F32)[:, u * P : (u + 1) * P], ident[:])
+            if pair + 2 < PAIRS:
+                load_w1_scales(nc.sync, pair + 2, 1)
+                w1.append(load_w1_words(pair + 2))
+            hs = ring.tile([P, 2, PAIR_SLOTS], F32, name="hs", bufs=4)
+            nc.scalar.copy(hs[:], tr[:])
+            cols = list1[:, pair * PAIR_SLOTS // 16 : (pair + 1) * PAIR_SLOTS // 16]
+            for u in range(2):
+                nc.vector.tensor_copy(cw[u][:].indirect(cols), hs[:, u, :])
+
+        w2 = keep.tile([P, E2, 2 * N], U8, name="w2", tag="even", align_bytes=64)
+        nc.sync.dma_start(w2[:].bitcast(I32), w2_words[:, 0].rearrange("f p b -> p f b").bitcast(I32))
+        src = w2_scales[:, 0].rearrange("f (q r) n -> r q f n", r=4)
+        for r in range(4):
+            dst = ws[r:P:32, 0 : E2 * N].bitcast(I32)
+            nc.sync.dma_start(dst.rearrange("q (f n) -> q f n", f=E2), src[r].bitcast(I32))
+
+        res = keep.tile([P, T], F32, name="res")
+        woven = {}
+        sums = {}
+
+        def gather2(f):
+            cols = list2[:, f * C2 // 16 : (f + 1) * C2 // 16]
+            cg = ring.tile([P, 2, C2], U32, name="cg", bufs=4)
+            for u in range(2):
+                nc.vector.tensor_copy(cg[:, u, :], cw[u][:].bitcast(U32).indirect(cols))
+            cq = ring.tile([P, 4 * C2], BF16, name="cq", bufs=4, align_bytes=64)
+            nc.scalar.copy(cq[:].bitcast(U32).rearrange("p (m u) -> p m u", u=2), cg[:].rearrange("p u m -> p m u"))
+            woven[f] = cq
+
+        def multiply2(f):
+            codes = ring.tile([P, C2], U32, name="codes", bufs=4, align_bytes=64)
+            scales = ring.tile([P, C2], U8, name="scales", bufs=4, align_bytes=64)
+            nc.vector.quantize_mx(out=codes[:].bitcast(FP8X4), scales=scales[:], in_=woven[f][:])
+            y = psum.tile([P, C2], F32, name="y", tag="y")
+            nc.tensor.matmul_mx(
+                out=y[:],
+                lhsT=w2[:, f, :].bitcast(FP4X4),
+                lhsT_scale=ws[:, f * N : (f + 1) * N],
+                rhs=codes[:].bitcast(FP8X4),
+                rhs_scale=scales[:],
+                start=True,
+                stop=True,
+            )
+            ys = ring.tile([P, C2], F32, name="ys", bufs=4)
+            nc.scalar.copy(ys[:], y[:])
+            sums[f] = ys
+
+        def scatter2(f):
+            cols = list2[:, f * C2 // 16 : (f + 1) * C2 // 16]
+            nc.vector.tensor_tensor(res[:].indirect(cols), sums[f][:], g2[:, f * C2 : (f + 1) * C2], MULT)
+
+        for step in range(E2 + 3):
+            if step < E2:
+                gather2(step)
+            if 3 <= step:
+                scatter2(step - 3)
+            if 1 <= step <= E2:
+                multiply2(step - 1)
+
+        nc.sync.dma_start(out, res[:])

@@ -42,42 +42,44 @@ def tile_moe_ser_none_kernel(
         xs = keep.tile([P, T], U8, name="xs", tag="odd", align_bytes=64)
         nc.gpsimd.memset(xs[:].bitcast(I32), 0)
         for s in range(PASSES):
-            nc.scalar.dma_start(xs[s:64:4, :].bitcast(I32), x_scales[s].bitcast(I32))
+            nc.sync.dma_start(xs[s:64:4, :].bitcast(I32), x_scales[s].bitcast(I32))
 
         grow = keep.tile([P, P], F32, name="grow")
         nc.gpsimd.memset(grow[:], 0.0)
-        nc.scalar.dma_start(grow[0:E1, :], gate1[0].rearrange("(e c) -> e c", e=E1))
+        nc.gpsimd.dma_start(grow[0:E1, :], gate1[0].rearrange("(e c) -> e c", e=E1))
 
-        xw = []
-        for s in range(PASSES):
-            t = keep.tile([P, T], I32, name="xw%d" % s, tag="xw%d" % s)
-            nc.sync.dma_start(t[:], x_words[s].rearrange("p t d -> p (t d)").bitcast(I32))
-            xw.append(t)
+        x_first = keep.tile([P, T], I32, name="x_first")
+        nc.sync.dma_start(x_first[:], x_words[0].rearrange("p t d -> p (t d)").bitcast(I32))
+        x_rest = keep.tile([P, PASSES - 1, T], I32, name="x_rest", tag="x_rest")
+        nc.sync.dma_start(x_rest[:], x_words[1:].rearrange("s p t d -> p s (t d)").bitcast(I32))
 
-        ws = keep.tile([P, 2 * PAIR_PLANES * H], U8, name="ws", align_bytes=64)
-        nc.vector.memset(ws[:].bitcast(I32), 0)
-        xp = keep.tile([P, 4 * T], U8, name="xp", align_bytes=64)
-        nc.vector.memset(xp[:].bitcast(I32), 0)
-
-        def load_w1_scales(queue, first_pair, pairs):
-            src = w1_scales[2 * first_pair : 2 * (first_pair + pairs)].rearrange("e s (q r) i -> r q (e s) i", r=4)
-            c0 = (first_pair % 2) * PAIR_PLANES * H
-            for r in range(4):
-                dst = ws[r:P:32, c0 : c0 + pairs * PAIR_PLANES * H].bitcast(I32)
-                queue.dma_start(dst.rearrange("q (g i) -> q g i", i=H // 4), src[r].bitcast(I32))
-
-        def load_w1_words(pair):
-            t = keep.tile([P, PAIR_PLANES, 2 * H], U8, name="w1_%d" % pair, tag=("even", "odd")[pair % 2], align_bytes=64)
-            src = w1_words[2 * pair : 2 * pair + 2].rearrange("e s p b -> p (e s) b")
-            nc.sync.dma_start(t[:].bitcast(I32), src.bitcast(I32))
+        def zeroed_plane(engine, name, width, read):
+            t = keep.tile([P, width], U8, name=name, align_bytes=64)
+            engine.memset(t[:, :read].bitcast(I32), 0)
             return t
 
-        w1 = [load_w1_words(0)]
-        load_w1_scales(nc.scalar, 0, 2)
+        ws_first = zeroed_plane(nc.vector, "ws_first", PAIR_PLANES * H, PAIR_PLANES * H)
+        xp = zeroed_plane(nc.vector, "xp", 4 * T, PASSES * T)
+
+        def load_scales(queue, plane, src):
+            rows = src.rearrange("e s (q r) i -> r q (e s) i", r=4)
+            for r in range(4):
+                dst = plane[r:P:32, :].bitcast(I32).rearrange("q (g i) -> q g i", g=rows.shape[2])
+                queue.dma_start(dst, rows[r].bitcast(I32))
+
+        def load_w1_words(dst, pair):
+            src = w1_words[2 * pair : 2 * pair + 2].rearrange("e s p b -> p (e s) b")
+            nc.sync.dma_start(dst.bitcast(I32), src.bitcast(I32))
+
+        w_first = keep.tile([P, PAIR_PLANES, 2 * H], U8, name="w_first", align_bytes=64)
+        load_w1_words(w_first[:], 0)
+        load_scales(nc.scalar, ws_first, w1_scales[0:2])
 
         ident = keep.tile([P, P], F32, name="ident")
         make_identity(nc, ident[:])
-        nc.sync.dma_start(list2[:], offs2)
+        ws_second = zeroed_plane(nc.gpsimd, "ws_second", PAIR_PLANES * H, PAIR_PLANES * H)
+        ws_rest = zeroed_plane(nc.gpsimd, "ws_rest", 2 * PAIR_PLANES * H, 2 * PAIR_PLANES * H)
+        w2s = zeroed_plane(nc.gpsimd, "w2s", E2 * N, E2 * N)
         gps = psum.tile([P, P], F32, name="gps", tag="y")
         nc.tensor.transpose(gps[:], grow[:], ident[:])
         gcol = keep.tile([P, E1], F32, name="gcol")
@@ -90,62 +92,69 @@ def tile_moe_ser_none_kernel(
         for q in range(4):
             dst = xp[32 * q : 32 * q + 4, :].bitcast(I32).rearrange("r (s t) -> r s t", s=4)
             nc.scalar.dma_start(dst, xsg[16 * q : 16 * q + 16, :].bitcast(I32))
-        w1.append(load_w1_words(1))
+        w1 = [w_first[:]]
+        for pair in range(1, PAIRS):
+            tag = "odd" if pair == 1 else "w1_%d" % pair
+            w1.append(keep.tile([P, PAIR_PLANES, 2 * H], U8, name="w1_%d" % pair, tag=tag, align_bytes=64)[:])
+        load_w1_words(w1[1], 1)
+        load_scales(nc.sync, ws_second, w1_scales[2:4])
+        load_w1_words(w1[2], 2)
+        load_scales(nc.sync, ws_rest, w1_scales[4:8])
+        load_w1_words(w1[3], 3)
+        ws = [ws_first[:], ws_second[:], ws_rest[:, : PAIR_PLANES * H], ws_rest[:, PAIR_PLANES * H :]]
+        nc.sync.dma_start(list2[:], offs2)
+        w2 = keep.tile([P, E2, 2 * N], U8, name="w2", align_bytes=64)
+        nc.sync.dma_start(w2[:].bitcast(I32), w2_words[:, 0].rearrange("f p b -> p f b").bitcast(I32))
+        load_scales(nc.sync, w2s, w2_scales)
 
         xg = {}
         for half in range(2):
             cols = list1[:, half * HALF // 16 : (half + 1) * HALF // 16]
-            for s in range(PASSES):
-                t = keep.tile([P, HALF], U32, name="xg%d_%d" % (half, s), align_bytes=64)
-                nc.vector.tensor_copy(t[:], xw[s][:].bitcast(U32).indirect(cols))
-                xg[(half, s)] = t
+            t = keep.tile([P, HALF], U32, name="xg_first%d" % half, align_bytes=64)
+            nc.vector.tensor_copy(t[:], x_first[:].bitcast(U32).indirect(cols))
+            for j in range(E1 // 2):
+                xg[(half * E1 // 2 + j, 0)] = t[:, j * C1 : (j + 1) * C1]
+        for pair in range(PAIRS):
+            cols = list1[:, pair * PAIR_SLOTS // 16 : (pair + 1) * PAIR_SLOTS // 16]
+            for s in range(1, PASSES):
+                t = keep.tile([P, PAIR_SLOTS], U32, name="xg%d_%d" % (pair, s), align_bytes=64)
+                nc.vector.tensor_copy(t[:], x_rest[:, s - 1, :].bitcast(U32).indirect(cols))
+                for j in range(2):
+                    xg[(2 * pair + j, s)] = t[:, j * C1 : (j + 1) * C1]
 
-        g2 = keep.tile([P, T], F32, name="g2", tag="xw0")
+        g2 = keep.tile([P, T], F32, name="g2", tag="x_rest")
         nc.sync.dma_start(g2[:], gate2)
 
         cw = [keep.tile([P, T], F32, name="cw%d" % u) for u in range(2)]
-        for pair in range(PAIRS):
-            tr = psum.tile([P, 2, PAIR_SLOTS], F32, name="tr", tag="tr")
-            for j in range(2):
-                e = 2 * pair + j
-                half, col = divmod(e * C1, HALF)
-                h = psum.tile([P, H], F32, name="h", tag="h", bufs=4)
-                for s in range(PASSES):
-                    g = j * PASSES + s
-                    c0 = ((pair % 2) * PAIR_PLANES + g) * H
-                    nc.tensor.matmul_mx(
-                        out=h[:],
-                        lhsT=xg[(half, s)][:, col : col + C1].bitcast(FP8X4),
-                        lhsT_scale=xp[:, s * T + e * C1 : s * T + (e + 1) * C1],
-                        rhs=w1[pair][:, g, :].bitcast(FP4X4),
-                        rhs_scale=ws[:, c0 : c0 + H],
-                        start=(s == 0),
-                        stop=(s == PASSES - 1),
-                    )
-                hb = ring.tile([P, H], BF16, name="hb", bufs=4)
-                nc.scalar.activation(
-                    hb[:].rearrange("c (u p v) -> c u p v", u=2, v=2),
-                    h[:].rearrange("c (p u v) -> c u p v", u=2, v=2),
-                    COPY,
-                    scale=gcol[:, e : e + 1],
+        for e in range(E1):
+            pair, j = divmod(e, 2)
+            h = psum.tile([P, H], F32, name="h", tag="h")
+            for s in range(PASSES):
+                g = j * PASSES + s
+                nc.tensor.matmul_mx(
+                    out=h[:],
+                    lhsT=xg[(e, s)].bitcast(FP8X4),
+                    lhsT_scale=xp[:, s * T + e * C1 : s * T + (e + 1) * C1],
+                    rhs=w1[pair][:, g, :].bitcast(FP4X4),
+                    rhs_scale=ws[pair][:, g * H : (g + 1) * H],
+                    start=(s == 0),
+                    stop=(s == PASSES - 1),
                 )
-                for u in range(2):
-                    nc.tensor.transpose(tr[:, u, j * C1 : (j + 1) * C1], hb[:].bitcast(F32)[:, u * P : (u + 1) * P], ident[:])
-            if pair + 2 < PAIRS:
-                load_w1_scales(nc.sync, pair + 2, 1)
-                w1.append(load_w1_words(pair + 2))
-            hs = ring.tile([P, 2, PAIR_SLOTS], F32, name="hs", bufs=4)
+            hb = ring.tile([P, H], BF16, name="hb", bufs=4)
+            nc.scalar.activation(
+                hb[:].rearrange("c (u p v) -> c u p v", u=2, v=2),
+                h[:].rearrange("c (p u v) -> c u p v", u=2, v=2),
+                COPY,
+                scale=gcol[:, e : e + 1],
+            )
+            tr = psum.tile([P, 2, C1], F32, name="tr", tag="tr")
+            for u in range(2):
+                nc.tensor.transpose(tr[:, u, :], hb[:].bitcast(F32)[:, u * P : (u + 1) * P], ident[:])
+            hs = ring.tile([P, 2, C1], F32, name="hs", bufs=E1)
             nc.scalar.copy(hs[:], tr[:])
-            cols = list1[:, pair * PAIR_SLOTS // 16 : (pair + 1) * PAIR_SLOTS // 16]
+            cols = list1[:, e * C1 // 16 : (e + 1) * C1 // 16]
             for u in range(2):
                 nc.vector.tensor_copy(cw[u][:].indirect(cols), hs[:, u, :])
-
-        w2 = keep.tile([P, E2, 2 * N], U8, name="w2", tag="even", align_bytes=64)
-        nc.sync.dma_start(w2[:].bitcast(I32), w2_words[:, 0].rearrange("f p b -> p f b").bitcast(I32))
-        src = w2_scales[:, 0].rearrange("f (q r) n -> r q f n", r=4)
-        for r in range(4):
-            dst = ws[r:P:32, 0 : E2 * N].bitcast(I32)
-            nc.sync.dma_start(dst.rearrange("q (f n) -> q f n", f=E2), src[r].bitcast(I32))
 
         res = keep.tile([P, T], F32, name="res")
         woven = {}
@@ -168,7 +177,7 @@ def tile_moe_ser_none_kernel(
             nc.tensor.matmul_mx(
                 out=y[:],
                 lhsT=w2[:, f, :].bitcast(FP4X4),
-                lhsT_scale=ws[:, f * N : (f + 1) * N],
+                lhsT_scale=w2s[:, f * N : (f + 1) * N],
                 rhs=codes[:].bitcast(FP8X4),
                 rhs_scale=scales[:],
                 start=True,

@@ -46,66 +46,68 @@ def tile_moe_ser_none_kernel(
 
         grow = keep.tile([P, P], F32, name="grow")
         nc.gpsimd.memset(grow[:], 0.0)
-        nc.gpsimd.dma_start(grow[0:E1, :], gate1[0].rearrange("(e c) -> e c", e=E1))
+        nc.scalar.dma_start(grow[0:E1, :], gate1[0].rearrange("(e c) -> e c", e=E1))
 
         x_first = keep.tile([P, T], I32, name="x_first")
         nc.sync.dma_start(x_first[:], x_words[0].rearrange("p t d -> p (t d)").bitcast(I32))
         x_rest = keep.tile([P, PASSES - 1, T], I32, name="x_rest", tag="x_rest")
         nc.sync.dma_start(x_rest[:], x_words[1:].rearrange("s p t d -> p s (t d)").bitcast(I32))
 
-        def zeroed_plane(engine, name, width, read):
-            t = keep.tile([P, width], U8, name=name, align_bytes=64)
-            engine.memset(t[:, :read].bitcast(I32), 0)
-            return t
-
-        ws_first = zeroed_plane(nc.vector, "ws_first", PAIR_PLANES * H, PAIR_PLANES * H)
-        xp = zeroed_plane(nc.vector, "xp", 4 * T, PASSES * T)
+        ws = []
+        for slot in range(2):
+            ws.append(keep.tile([P, PAIR_PLANES * H], U8, name="ws%d" % slot, align_bytes=64))
+        parts = ((0, PAIR_SLOTS), (PAIR_SLOTS, T - PAIR_SLOTS))
+        xp = [keep.tile([P, 4, n], U8, name="xp%d" % first, align_bytes=64) for first, n in parts]
+        nc.vector.memset(ws[0][:].bitcast(I32), 0)
+        for plane in xp:
+            nc.vector.memset(plane[:, :PASSES, :].bitcast(I32), 0)
+        nc.vector.memset(ws[1][:].bitcast(I32), 0)
 
         def load_scales(queue, plane, src):
             rows = src.rearrange("e s (q r) i -> r q (e s) i", r=4)
+            width = rows.shape[2] * rows.shape[3]
             for r in range(4):
-                dst = plane[r:P:32, :].bitcast(I32).rearrange("q (g i) -> q g i", g=rows.shape[2])
+                dst = plane[r:P:32, :width].bitcast(I32).rearrange("q (g i) -> q g i", g=rows.shape[2])
                 queue.dma_start(dst, rows[r].bitcast(I32))
 
-        def load_w1_words(dst, pair):
-            src = w1_words[2 * pair : 2 * pair + 2].rearrange("e s p b -> p (e s) b")
-            nc.sync.dma_start(dst.bitcast(I32), src.bitcast(I32))
+        w1 = {}
 
-        w_first = keep.tile([P, PAIR_PLANES, 2 * H], U8, name="w_first", align_bytes=64)
-        load_w1_words(w_first[:], 0)
-        load_scales(nc.scalar, ws_first, w1_scales[0:2])
+        def load_w1_words(first, count, tag):
+            t = keep.tile([P, count * PASSES, 2 * H], U8, name="w1_%d" % first, tag=tag, align_bytes=64)
+            src = w1_words[first : first + count].rearrange("e s p b -> p (e s) b")
+            nc.sync.dma_start(t[:].bitcast(I32), src.bitcast(I32))
+            for j in range(count):
+                w1[first + j] = t[:, j * PASSES : (j + 1) * PASSES, :]
+
+        load_w1_words(0, 1, "w1_0")
+        load_w1_words(1, 1, "w1_1")
+        load_scales(nc.scalar, ws[0], w1_scales[0:2])
 
         ident = keep.tile([P, P], F32, name="ident")
         make_identity(nc, ident[:])
-        ws_second = zeroed_plane(nc.gpsimd, "ws_second", PAIR_PLANES * H, PAIR_PLANES * H)
-        ws_rest = zeroed_plane(nc.gpsimd, "ws_rest", 2 * PAIR_PLANES * H, 2 * PAIR_PLANES * H)
-        w2s = zeroed_plane(nc.gpsimd, "w2s", E2 * N, E2 * N)
+
+        def gather_scales(part):
+            first, n = parts[part]
+            xsg = keep.tile([P, n], U8, name="xsg%d" % part, align_bytes=64)
+            nc.vector.tensor_copy(xsg[:], xs[:].indirect(list1[:, first // 16 : (first + n) // 16]))
+            for q in range(4):
+                dst = xp[part][32 * q : 32 * q + 4, :, :].bitcast(I32)
+                nc.scalar.dma_start(dst, xsg[16 * q : 16 * q + 16, :].bitcast(I32))
+
+        gather_scales(0)
         gps = psum.tile([P, P], F32, name="gps", tag="y")
         nc.tensor.transpose(gps[:], grow[:], ident[:])
         gcol = keep.tile([P, E1], F32, name="gcol")
         nc.scalar.activation(gcol[:], gps[:, 0:E1], COPY)
+        gather_scales(1)
 
-        xsg = keep.tile([P, T], U8, name="xsg", align_bytes=64)
-        for half in range(2):
-            cols = list1[:, half * HALF // 16 : (half + 1) * HALF // 16]
-            nc.vector.tensor_copy(xsg[:, half * HALF : (half + 1) * HALF], xs[:].indirect(cols))
-        for q in range(4):
-            dst = xp[32 * q : 32 * q + 4, :].bitcast(I32).rearrange("r (s t) -> r s t", s=4)
-            nc.scalar.dma_start(dst, xsg[16 * q : 16 * q + 16, :].bitcast(I32))
-        w1 = [w_first[:]]
-        for pair in range(1, PAIRS):
-            tag = "odd" if pair == 1 else "w1_%d" % pair
-            w1.append(keep.tile([P, PAIR_PLANES, 2 * H], U8, name="w1_%d" % pair, tag=tag, align_bytes=64)[:])
-        load_w1_words(w1[1], 1)
-        load_scales(nc.sync, ws_second, w1_scales[2:4])
-        load_w1_words(w1[2], 2)
-        load_scales(nc.sync, ws_rest, w1_scales[4:8])
-        load_w1_words(w1[3], 3)
-        ws = [ws_first[:], ws_second[:], ws_rest[:, : PAIR_PLANES * H], ws_rest[:, PAIR_PLANES * H :]]
+        load_w1_words(2, 2, "odd")
+        load_scales(nc.sync, ws[1], w1_scales[2:4])
+        load_w1_words(4, 2, "w1_4")
+        load_w1_words(6, 2, "w1_6")
         nc.sync.dma_start(list2[:], offs2)
         w2 = keep.tile([P, E2, 2 * N], U8, name="w2", align_bytes=64)
         nc.sync.dma_start(w2[:].bitcast(I32), w2_words[:, 0].rearrange("f p b -> p f b").bitcast(I32))
-        load_scales(nc.sync, w2s, w2_scales)
 
         xg = {}
         for half in range(2):
@@ -128,18 +130,22 @@ def tile_moe_ser_none_kernel(
         cw = [keep.tile([P, T], F32, name="cw%d" % u) for u in range(2)]
         for e in range(E1):
             pair, j = divmod(e, 2)
+            part = min(pair, 1)
+            col = e * C1 - parts[part][0]
             h = psum.tile([P, H], F32, name="h", tag="h")
             for s in range(PASSES):
                 g = j * PASSES + s
                 nc.tensor.matmul_mx(
                     out=h[:],
                     lhsT=xg[(e, s)].bitcast(FP8X4),
-                    lhsT_scale=xp[:, s * T + e * C1 : s * T + (e + 1) * C1],
-                    rhs=w1[pair][:, g, :].bitcast(FP4X4),
-                    rhs_scale=ws[pair][:, g * H : (g + 1) * H],
+                    lhsT_scale=xp[part][:, s, col : col + C1],
+                    rhs=w1[e][:, s, :].bitcast(FP4X4),
+                    rhs_scale=ws[pair % 2][:, g * H : (g + 1) * H],
                     start=(s == 0),
                     stop=(s == PASSES - 1),
                 )
+            if j == 1 and pair + 2 < PAIRS:
+                load_scales(nc.sync, ws[pair % 2], w1_scales[2 * pair + 4 : 2 * pair + 6])
             hb = ring.tile([P, H], BF16, name="hb", bufs=4)
             nc.scalar.activation(
                 hb[:].rearrange("c (u p v) -> c u p v", u=2, v=2),
@@ -156,47 +162,41 @@ def tile_moe_ser_none_kernel(
             for u in range(2):
                 nc.vector.tensor_copy(cw[u][:].indirect(cols), hs[:, u, :])
 
-        res = keep.tile([P, T], F32, name="res")
-        woven = {}
-        sums = {}
+        load_scales(nc.sync, ws[0], w2_scales)
 
-        def gather2(f):
-            cols = list2[:, f * C2 // 16 : (f + 1) * C2 // 16]
-            cg = ring.tile([P, 2, C2], U32, name="cg", bufs=4)
+        gathered = []
+        for half in range(2):
+            cols = list2[:, half * HALF // 16 : (half + 1) * HALF // 16]
+            cg = ring.tile([P, 2, HALF], U32, name="cg")
             for u in range(2):
                 nc.vector.tensor_copy(cg[:, u, :], cw[u][:].bitcast(U32).indirect(cols))
-            cq = ring.tile([P, 4 * C2], BF16, name="cq", bufs=4, align_bytes=64)
-            nc.scalar.copy(cq[:].bitcast(U32).rearrange("p (m u) -> p m u", u=2), cg[:].rearrange("p u m -> p m u"))
-            woven[f] = cq
+            gathered.append(cg)
 
-        def multiply2(f):
-            codes = ring.tile([P, C2], U32, name="codes", bufs=4, align_bytes=64)
-            scales = ring.tile([P, C2], U8, name="scales", bufs=4, align_bytes=64)
-            nc.vector.quantize_mx(out=codes[:].bitcast(FP8X4), scales=scales[:], in_=woven[f][:])
+        res = keep.tile([P, T], F32, name="res")
+        ys = keep.tile([P, T], F32, name="ys")
+        for f in range(E2):
+            half, j = divmod(f, 2)
+            cq = ring.tile([P, 4 * C2], BF16, name="cq", bufs=E2, align_bytes=64)
+            pairs = gathered[half][:, :, j * C2 : (j + 1) * C2].rearrange("p u m -> p m u")
+            nc.scalar.copy(cq[:].bitcast(U32).rearrange("p (m u) -> p m u", u=2), pairs)
+            codes = ring.tile([P, C2], U32, name="codes", bufs=E2, align_bytes=64)
+            scales = ring.tile([P, C2], U8, name="scales", bufs=E2, align_bytes=64)
+            nc.vector.quantize_mx(out=codes[:].bitcast(FP8X4), scales=scales[:], in_=cq[:])
             y = psum.tile([P, C2], F32, name="y", tag="y")
             nc.tensor.matmul_mx(
                 out=y[:],
                 lhsT=w2[:, f, :].bitcast(FP4X4),
-                lhsT_scale=w2s[:, f * N : (f + 1) * N],
+                lhsT_scale=ws[0][:, f * N : (f + 1) * N],
                 rhs=codes[:].bitcast(FP8X4),
                 rhs_scale=scales[:],
                 start=True,
                 stop=True,
             )
-            ys = ring.tile([P, C2], F32, name="ys", bufs=4)
-            nc.scalar.copy(ys[:], y[:])
-            sums[f] = ys
+            nc.scalar.copy(ys[:, f * C2 : (f + 1) * C2], y[:])
 
-        def scatter2(f):
-            cols = list2[:, f * C2 // 16 : (f + 1) * C2 // 16]
-            nc.vector.tensor_tensor(res[:].indirect(cols), sums[f][:], g2[:, f * C2 : (f + 1) * C2], MULT)
-
-        for step in range(E2 + 3):
-            if step < E2:
-                gather2(step)
-            if 3 <= step:
-                scatter2(step - 3)
-            if 1 <= step <= E2:
-                multiply2(step - 1)
+        for half in range(2):
+            cols = list2[:, half * HALF // 16 : (half + 1) * HALF // 16]
+            slots = slice(half * HALF, (half + 1) * HALF)
+            nc.vector.tensor_tensor(res[:].indirect(cols), ys[:, slots], g2[:, slots], MULT)
 
         nc.sync.dma_start(out, res[:])

@@ -54,14 +54,15 @@ def tile_moe_ser_none_kernel(
         nc.sync.dma_start(x_rest[:], x_words[1:].rearrange("s p t d -> p s (t d)").bitcast(I32))
 
         ws = []
-        for slot in range(2):
+        for slot in range(3):
             ws.append(keep.tile([P, PAIR_PLANES * H], U8, name="ws%d" % slot, align_bytes=64))
         parts = ((0, PAIR_SLOTS), (PAIR_SLOTS, T - PAIR_SLOTS))
         xp = [keep.tile([P, 4, n], U8, name="xp%d" % first, align_bytes=64) for first, n in parts]
         nc.vector.memset(ws[0][:].bitcast(I32), 0)
         for plane in xp:
             nc.vector.memset(plane[:, :PASSES, :].bitcast(I32), 0)
-        nc.vector.memset(ws[1][:].bitcast(I32), 0)
+        for plane in ws[1:]:
+            nc.vector.memset(plane[:].bitcast(I32), 0)
 
         def load_scales(queue, plane, src):
             rows = src.rearrange("e s (q r) i -> r q (e s) i", r=4)
@@ -104,10 +105,8 @@ def tile_moe_ser_none_kernel(
         load_w1_words(2, 2, "odd")
         load_scales(nc.sync, ws[1], w1_scales[2:4])
         load_w1_words(4, 2, "w1_4")
+        load_scales(nc.sync, ws[2], w1_scales[4:6])
         load_w1_words(6, 2, "w1_6")
-        nc.sync.dma_start(list2[:], offs2)
-        w2 = keep.tile([P, E2, 2 * N], U8, name="w2", align_bytes=64)
-        nc.sync.dma_start(w2[:].bitcast(I32), w2_words[:, 0].rearrange("f p b -> p f b").bitcast(I32))
 
         xg = {}
         for half in range(2):
@@ -124,9 +123,6 @@ def tile_moe_ser_none_kernel(
                 for j in range(2):
                     xg[(2 * pair + j, s)] = t[:, j * C1 : (j + 1) * C1]
 
-        g2 = keep.tile([P, T], F32, name="g2", tag="x_rest")
-        nc.sync.dma_start(g2[:], gate2)
-
         cw = [keep.tile([P, T], F32, name="cw%d" % u) for u in range(2)]
         for e in range(E1):
             pair, j = divmod(e, 2)
@@ -140,12 +136,12 @@ def tile_moe_ser_none_kernel(
                     lhsT=xg[(e, s)].bitcast(FP8X4),
                     lhsT_scale=xp[part][:, s, col : col + C1],
                     rhs=w1[e][:, s, :].bitcast(FP4X4),
-                    rhs_scale=ws[pair % 2][:, g * H : (g + 1) * H],
+                    rhs_scale=ws[pair % 3][:, g * H : (g + 1) * H],
                     start=(s == 0),
                     stop=(s == PASSES - 1),
                 )
-            if j == 1 and pair + 2 < PAIRS:
-                load_scales(nc.sync, ws[pair % 2], w1_scales[2 * pair + 4 : 2 * pair + 6])
+            if e == 1:
+                load_scales(nc.sync, ws[0], w1_scales[6:8])
             hb = ring.tile([P, H], BF16, name="hb", bufs=4)
             nc.scalar.activation(
                 hb[:].rearrange("c (u p v) -> c u p v", u=2, v=2),
@@ -162,31 +158,36 @@ def tile_moe_ser_none_kernel(
             for u in range(2):
                 nc.vector.tensor_copy(cw[u][:].indirect(cols), hs[:, u, :])
 
-        load_scales(nc.sync, ws[0], w2_scales)
+        nc.sync.dma_start(list2[:], offs2)
+        w2 = keep.tile([P, E2, 2 * N], U8, name="w2", align_bytes=64)
+        nc.sync.dma_start(w2[:].bitcast(I32), w2_words[:, 0].rearrange("f p b -> p f b").bitcast(I32))
+        load_scales(nc.sync, ws[1], w2_scales)
+        g2 = keep.tile([P, T], F32, name="g2", tag="x_rest")
+        nc.sync.dma_start(g2[:], gate2)
 
-        gathered = []
-        for half in range(2):
-            cols = list2[:, half * HALF // 16 : (half + 1) * HALF // 16]
-            cg = ring.tile([P, 2, HALF], U32, name="cg")
-            for u in range(2):
-                nc.vector.tensor_copy(cg[:, u, :], cw[u][:].bitcast(U32).indirect(cols))
-            gathered.append(cg)
 
         res = keep.tile([P, T], F32, name="res")
         ys = keep.tile([P, T], F32, name="ys")
-        for f in range(E2):
-            half, j = divmod(f, 2)
+        woven = []
+
+        def gather2(f):
+            cols = list2[:, f * C2 // 16 : (f + 1) * C2 // 16]
+            cg = ring.tile([P, 2, C2], U32, name="cg")
+            for u in range(2):
+                nc.vector.tensor_copy(cg[:, u, :], cw[u][:].bitcast(U32).indirect(cols))
             cq = ring.tile([P, 4 * C2], BF16, name="cq", bufs=E2, align_bytes=64)
-            pairs = gathered[half][:, :, j * C2 : (j + 1) * C2].rearrange("p u m -> p m u")
-            nc.scalar.copy(cq[:].bitcast(U32).rearrange("p (m u) -> p m u", u=2), pairs)
+            nc.scalar.copy(cq[:].bitcast(U32).rearrange("p (m u) -> p m u", u=2), cg[:].rearrange("p u m -> p m u"))
+            woven.append(cq)
+
+        def multiply2(f):
             codes = ring.tile([P, C2], U32, name="codes", bufs=E2, align_bytes=64)
             scales = ring.tile([P, C2], U8, name="scales", bufs=E2, align_bytes=64)
-            nc.vector.quantize_mx(out=codes[:].bitcast(FP8X4), scales=scales[:], in_=cq[:])
+            nc.vector.quantize_mx(out=codes[:].bitcast(FP8X4), scales=scales[:], in_=woven[f][:])
             y = psum.tile([P, C2], F32, name="y", tag="y")
             nc.tensor.matmul_mx(
                 out=y[:],
                 lhsT=w2[:, f, :].bitcast(FP4X4),
-                lhsT_scale=ws[0][:, f * N : (f + 1) * N],
+                lhsT_scale=ws[1][:, f * N : (f + 1) * N],
                 rhs=codes[:].bitcast(FP8X4),
                 rhs_scale=scales[:],
                 start=True,
@@ -194,9 +195,17 @@ def tile_moe_ser_none_kernel(
             )
             nc.scalar.copy(ys[:, f * C2 : (f + 1) * C2], y[:])
 
-        for half in range(2):
-            cols = list2[:, half * HALF // 16 : (half + 1) * HALF // 16]
-            slots = slice(half * HALF, (half + 1) * HALF)
+        def scatter2(f):
+            slots = slice(f * C2, (f + 1) * C2)
+            cols = list2[:, slots.start // 16 : slots.stop // 16]
             nc.vector.tensor_tensor(res[:].indirect(cols), ys[:, slots], g2[:, slots], MULT)
+
+        gather2(0)
+        for f in range(1, E2):
+            gather2(f)
+            multiply2(f - 1)
+        multiply2(E2 - 1)
+        for f in range(E2):
+            scatter2(f)
 
         nc.sync.dma_start(out, res[:])

@@ -3,7 +3,9 @@ from contextlib import ExitStack
 import concourse.mybir as mybir
 from concourse.masks import make_identity
 
-K, T, E1, C1, E2, C2, H, N = 1536, 1024, 8, 128, 4, 256, 512, 128
+K, T, H, N = 1536, 1024, 512, 128
+E1, C1 = 8, 128
+E2, C2 = 4, 256
 FLOPS = 2 * T * K * H + 2 * T * H * N
 
 F32 = mybir.dt.float32
@@ -19,10 +21,13 @@ MULT = mybir.AluOpType.mult
 
 P = 128
 PASSES = K // 512
-PAIRS = E1 // 2
-PAIR_SLOTS = 2 * C1
-HALF = T // 2
-PAIR_PLANES = 2 * PASSES
+QUADRANT = 32
+LIVE = 4
+PER_COLUMN = 16
+ROWS = 4
+COUPLES = E1 // 2
+COUPLE_SLOTS = 2 * C1
+SCALE_TILES = 3
 
 
 def tile_moe_ser_none_kernel(
@@ -35,151 +40,152 @@ def tile_moe_ser_none_kernel(
         ring = ctx.enter_context(tc.tile_pool(name="ring", bufs=2))
         psum = ctx.enter_context(tc.psum_pool(name="psum", bufs=2))
 
-        list1 = lists.tile([P, T // 16], U16, name="list1")
-        list2 = lists.tile([P, T // 16], U16, name="list2")
+        list1 = lists.tile([P, T // PER_COLUMN], U16, name="list1")
+        list2 = lists.tile([P, T // PER_COLUMN], U16, name="list2")
         nc.sync.dma_start(list1[:], offs)
 
-        xs = keep.tile([P, T], U8, name="xs", tag="odd", align_bytes=64)
+        def entries(list_tile, first, count):
+            return list_tile[:, first // PER_COLUMN : (first + count) // PER_COLUMN]
+
+        xs = keep.tile([P, T], U8, name="xs", tag="xs_then_w1", align_bytes=64)
         nc.gpsimd.memset(xs[:].bitcast(I32), 0)
         for s in range(PASSES):
-            nc.sync.dma_start(xs[s:64:4, :].bitcast(I32), x_scales[s].bitcast(I32))
+            nc.sync.dma_start(xs[s : 16 * ROWS : ROWS, :].bitcast(I32), x_scales[s].bitcast(I32))
 
-        grow = keep.tile([P, P], F32, name="grow")
-        nc.gpsimd.memset(grow[:], 0.0)
-        nc.scalar.dma_start(grow[0:E1, :], gate1[0].rearrange("(e c) -> e c", e=E1))
+        gate_rows = keep.tile([P, P], F32, name="gate_rows")
+        nc.gpsimd.memset(gate_rows[:], 0.0)
+        nc.scalar.dma_start(gate_rows[0:E1, :], gate1[0].rearrange("(e c) -> e c", e=E1))
 
         x_first = keep.tile([P, T], I32, name="x_first")
         nc.sync.dma_start(x_first[:], x_words[0].rearrange("p t d -> p (t d)").bitcast(I32))
-        x_rest = keep.tile([P, PASSES - 1, T], I32, name="x_rest", tag="x_rest")
+        x_rest = keep.tile([P, PASSES - 1, T], I32, name="x_rest", tag="x_rest_then_gate2")
         nc.sync.dma_start(x_rest[:], x_words[1:].rearrange("s p t d -> p s (t d)").bitcast(I32))
 
         ws = []
-        for slot in range(3):
-            ws.append(keep.tile([P, PAIR_PLANES * H], U8, name="ws%d" % slot, align_bytes=64))
-        parts = ((0, PAIR_SLOTS), (PAIR_SLOTS, T - PAIR_SLOTS))
-        xp = [keep.tile([P, 4, n], U8, name="xp%d" % first, align_bytes=64) for first, n in parts]
+        for i in range(SCALE_TILES):
+            ws.append(keep.tile([P, 2 * PASSES * H], U8, name="ws%d" % i, align_bytes=64))
+        parts = ((0, COUPLE_SLOTS), (COUPLE_SLOTS, T - COUPLE_SLOTS))
+        xp = [keep.tile([P, ROWS, count], U8, name="xp%d" % first, align_bytes=64) for first, count in parts]
         nc.vector.memset(ws[0][:].bitcast(I32), 0)
-        for plane in xp:
-            nc.vector.memset(plane[:, :PASSES, :].bitcast(I32), 0)
-        for plane in ws[1:]:
-            nc.vector.memset(plane[:].bitcast(I32), 0)
+        for planes in xp:
+            nc.vector.memset(planes[:, :PASSES, :].bitcast(I32), 0)
+        for planes in ws[1:]:
+            nc.vector.memset(planes[:].bitcast(I32), 0)
 
-        def load_scales(queue, plane, src):
-            rows = src.rearrange("e s (q r) i -> r q (e s) i", r=4)
+        def load_scales(queue, planes, src):
+            rows = src.rearrange("e s (q r) i -> r q (e s) i", r=LIVE)
             width = rows.shape[2] * rows.shape[3]
-            for r in range(4):
-                dst = plane[r:P:32, :width].bitcast(I32).rearrange("q (g i) -> q g i", g=rows.shape[2])
+            for r in range(LIVE):
+                dst = planes[r:P:QUADRANT, :width].bitcast(I32).rearrange("q (g i) -> q g i", g=rows.shape[2])
                 queue.dma_start(dst, rows[r].bitcast(I32))
 
-        w1 = {}
+        w1 = []
 
-        def load_w1_words(first, count, tag):
-            t = keep.tile([P, count * PASSES, 2 * H], U8, name="w1_%d" % first, tag=tag, align_bytes=64)
-            src = w1_words[first : first + count].rearrange("e s p b -> p (e s) b")
-            nc.sync.dma_start(t[:].bitcast(I32), src.bitcast(I32))
-            for j in range(count):
-                w1[first + j] = t[:, j * PASSES : (j + 1) * PASSES, :]
+        def load_w1_words(tag):
+            e = len(w1)
+            words = keep.tile([P, PASSES, 2 * H], U8, name="w1_%d" % e, tag=tag, align_bytes=64)
+            nc.sync.dma_start(words[:].bitcast(I32), w1_words[e].rearrange("s p b -> p s b").bitcast(I32))
+            w1.append(words)
 
-        load_w1_words(0, 1, "w1_0")
-        load_w1_words(1, 1, "w1_1")
+        load_w1_words("w1_0")
+        load_w1_words("w1_1")
         load_scales(nc.scalar, ws[0], w1_scales[0:2])
 
         ident = keep.tile([P, P], F32, name="ident")
         make_identity(nc, ident[:])
 
-        def gather_scales(part):
-            first, n = parts[part]
-            xsg = keep.tile([P, n], U8, name="xsg%d" % part, align_bytes=64)
-            nc.vector.tensor_copy(xsg[:], xs[:].indirect(list1[:, first // 16 : (first + n) // 16]))
-            for q in range(4):
-                dst = xp[part][32 * q : 32 * q + 4, :, :].bitcast(I32)
-                nc.scalar.dma_start(dst, xsg[16 * q : 16 * q + 16, :].bitcast(I32))
+        def gather_scales(part, queue):
+            first, count = parts[part]
+            picked = keep.tile([P, count], U8, name="picked%d" % part, align_bytes=64)
+            nc.vector.tensor_copy(picked[:], xs[:].indirect(entries(list1, first, count)))
+            for q in range(P // QUADRANT):
+                dst = xp[part][QUADRANT * q : QUADRANT * q + LIVE, :, :].bitcast(I32)
+                queue.dma_start(dst, picked[LIVE * ROWS * q : LIVE * ROWS * (q + 1), :].bitcast(I32))
 
-        gather_scales(0)
-        gps = psum.tile([P, P], F32, name="gps", tag="y")
-        nc.tensor.transpose(gps[:], grow[:], ident[:])
-        gcol = keep.tile([P, E1], F32, name="gcol")
-        nc.scalar.activation(gcol[:], gps[:, 0:E1], COPY)
-        gather_scales(1)
+        gather_scales(0, nc.scalar)
+        gate_bank = psum.tile([P, P], F32, name="gate_bank", tag="y")
+        nc.tensor.transpose(gate_bank[:], gate_rows[:], ident[:])
+        gate_cols = keep.tile([P, E1], F32, name="gate_cols")
+        nc.scalar.activation(gate_cols[:], gate_bank[:, 0:E1], COPY)
+        gather_scales(1, nc.sync)
 
-        load_w1_words(2, 2, "odd")
-        load_scales(nc.sync, ws[1], w1_scales[2:4])
-        load_w1_words(4, 2, "w1_4")
-        load_scales(nc.sync, ws[2], w1_scales[4:6])
-        load_w1_words(6, 2, "w1_6")
+        for couple in range(1, COUPLES):
+            load_w1_words("xs_then_w1" if couple == 1 else "w1_%d" % (2 * couple))
+            if couple < SCALE_TILES:
+                load_scales(nc.sync, ws[couple], w1_scales[2 * couple : 2 * couple + 2])
+            load_w1_words("w1_%d" % (2 * couple + 1))
 
         xg = {}
-        for half in range(2):
-            cols = list1[:, half * HALF // 16 : (half + 1) * HALF // 16]
-            t = keep.tile([P, HALF], U32, name="xg_first%d" % half, align_bytes=64)
-            nc.vector.tensor_copy(t[:], x_first[:].bitcast(U32).indirect(cols))
+        for first in range(0, T, T // 2):
+            words = keep.tile([P, T // 2], U32, name="xg_first%d" % first, align_bytes=64)
+            nc.vector.tensor_copy(words[:], x_first[:].bitcast(U32).indirect(entries(list1, first, T // 2)))
             for j in range(E1 // 2):
-                xg[(half * E1 // 2 + j, 0)] = t[:, j * C1 : (j + 1) * C1]
-        for pair in range(PAIRS):
-            cols = list1[:, pair * PAIR_SLOTS // 16 : (pair + 1) * PAIR_SLOTS // 16]
+                xg[(first // C1 + j, 0)] = words[:, j * C1 : (j + 1) * C1]
+        for couple in range(COUPLES):
+            offsets = entries(list1, couple * COUPLE_SLOTS, COUPLE_SLOTS)
             for s in range(1, PASSES):
-                t = keep.tile([P, PAIR_SLOTS], U32, name="xg%d_%d" % (pair, s), align_bytes=64)
-                nc.vector.tensor_copy(t[:], x_rest[:, s - 1, :].bitcast(U32).indirect(cols))
+                words = keep.tile([P, COUPLE_SLOTS], U32, name="xg%d_%d" % (couple, s), align_bytes=64)
+                nc.vector.tensor_copy(words[:], x_rest[:, s - 1, :].bitcast(U32).indirect(offsets))
                 for j in range(2):
-                    xg[(2 * pair + j, s)] = t[:, j * C1 : (j + 1) * C1]
+                    xg[(2 * couple + j, s)] = words[:, j * C1 : (j + 1) * C1]
 
-        cw = [keep.tile([P, T], F32, name="cw%d" % u) for u in range(2)]
+        c_pairs = [keep.tile([P, T], F32, name="c_pairs%d" % u) for u in range(2)]
         for e in range(E1):
-            pair, j = divmod(e, 2)
-            part = min(pair, 1)
-            col = e * C1 - parts[part][0]
+            couple, j = divmod(e, 2)
+            part = min(couple, 1)
+            column = e * C1 - parts[part][0]
             h = psum.tile([P, H], F32, name="h", tag="h")
             for s in range(PASSES):
-                g = j * PASSES + s
+                plane = j * PASSES + s
                 nc.tensor.matmul_mx(
                     out=h[:],
                     lhsT=xg[(e, s)].bitcast(FP8X4),
-                    lhsT_scale=xp[part][:, s, col : col + C1],
+                    lhsT_scale=xp[part][:, s, column : column + C1],
                     rhs=w1[e][:, s, :].bitcast(FP4X4),
-                    rhs_scale=ws[pair % 3][:, g * H : (g + 1) * H],
+                    rhs_scale=ws[couple % SCALE_TILES][:, plane * H : (plane + 1) * H],
                     start=(s == 0),
                     stop=(s == PASSES - 1),
                 )
             if e == 1:
-                load_scales(nc.sync, ws[0], w1_scales[6:8])
-            hb = ring.tile([P, H], BF16, name="hb", bufs=4)
+                load_scales(nc.sync, ws[0], w1_scales[E1 - 2 : E1])
+
+            gated = ring.tile([P, H], BF16, name="gated", bufs=E1 // 2)
             nc.scalar.activation(
-                hb[:].rearrange("c (u p v) -> c u p v", u=2, v=2),
+                gated[:].rearrange("c (u p v) -> c u p v", u=2, v=2),
                 h[:].rearrange("c (p u v) -> c u p v", u=2, v=2),
                 COPY,
-                scale=gcol[:, e : e + 1],
+                scale=gate_cols[:, e : e + 1],
             )
-            tr = psum.tile([P, 2, C1], F32, name="tr", tag="tr")
+            turned = psum.tile([P, 2, C1], F32, name="turned", tag="turned")
             for u in range(2):
-                nc.tensor.transpose(tr[:, u, :], hb[:].bitcast(F32)[:, u * P : (u + 1) * P], ident[:])
-            hs = ring.tile([P, 2, C1], F32, name="hs", bufs=E1)
-            nc.scalar.copy(hs[:], tr[:])
-            cols = list1[:, e * C1 // 16 : (e + 1) * C1 // 16]
+                nc.tensor.transpose(turned[:, u, :], gated[:].bitcast(F32)[:, u * P : (u + 1) * P], ident[:])
+            staged = ring.tile([P, 2, C1], F32, name="staged", bufs=E1)
+            nc.scalar.copy(staged[:], turned[:])
             for u in range(2):
-                nc.vector.tensor_copy(cw[u][:].indirect(cols), hs[:, u, :])
+                nc.vector.tensor_copy(c_pairs[u][:].indirect(entries(list1, e * C1, C1)), staged[:, u, :])
 
         nc.sync.dma_start(list2[:], offs2)
         w2 = keep.tile([P, E2, 2 * N], U8, name="w2", align_bytes=64)
         nc.sync.dma_start(w2[:].bitcast(I32), w2_words[:, 0].rearrange("f p b -> p f b").bitcast(I32))
         load_scales(nc.sync, ws[1], w2_scales)
-        g2 = keep.tile([P, T], F32, name="g2", tag="x_rest")
+        g2 = keep.tile([P, T], F32, name="g2", tag="x_rest_then_gate2")
         nc.sync.dma_start(g2[:], gate2)
 
-
-        res = keep.tile([P, T], F32, name="res")
+        result = keep.tile([P, T], F32, name="result")
         ys = keep.tile([P, T], F32, name="ys")
         woven = []
 
-        def gather2(f):
-            cols = list2[:, f * C2 // 16 : (f + 1) * C2 // 16]
-            cg = ring.tile([P, 2, C2], U32, name="cg")
+        def gather_c(f):
+            pairs = ring.tile([P, 2, C2], U32, name="pairs")
             for u in range(2):
-                nc.vector.tensor_copy(cg[:, u, :], cw[u][:].bitcast(U32).indirect(cols))
-            cq = ring.tile([P, 4 * C2], BF16, name="cq", bufs=E2, align_bytes=64)
-            nc.scalar.copy(cq[:].bitcast(U32).rearrange("p (m u) -> p m u", u=2), cg[:].rearrange("p u m -> p m u"))
-            woven.append(cq)
+                nc.vector.tensor_copy(pairs[:, u, :], c_pairs[u][:].bitcast(U32).indirect(entries(list2, f * C2, C2)))
+            values = ring.tile([P, 4 * C2], BF16, name="values", bufs=E2, align_bytes=64)
+            nc.scalar.copy(
+                values[:].bitcast(U32).rearrange("p (m u) -> p m u", u=2), pairs[:].rearrange("p u m -> p m u")
+            )
+            woven.append(values)
 
-        def multiply2(f):
+        def multiply(f):
             codes = ring.tile([P, C2], U32, name="codes", bufs=E2, align_bytes=64)
             scales = ring.tile([P, C2], U8, name="scales", bufs=E2, align_bytes=64)
             nc.vector.quantize_mx(out=codes[:].bitcast(FP8X4), scales=scales[:], in_=woven[f][:])
@@ -195,17 +201,13 @@ def tile_moe_ser_none_kernel(
             )
             nc.scalar.copy(ys[:, f * C2 : (f + 1) * C2], y[:])
 
-        def scatter2(f):
-            slots = slice(f * C2, (f + 1) * C2)
-            cols = list2[:, slots.start // 16 : slots.stop // 16]
-            nc.vector.tensor_tensor(res[:].indirect(cols), ys[:, slots], g2[:, slots], MULT)
-
-        gather2(0)
+        gather_c(0)
         for f in range(1, E2):
-            gather2(f)
-            multiply2(f - 1)
-        multiply2(E2 - 1)
+            gather_c(f)
+            multiply(f - 1)
+        multiply(E2 - 1)
         for f in range(E2):
-            scatter2(f)
+            slots = slice(f * C2, (f + 1) * C2)
+            nc.vector.tensor_tensor(result[:].indirect(entries(list2, f * C2, C2)), ys[:, slots], g2[:, slots], MULT)
 
-        nc.sync.dma_start(out, res[:])
+        nc.sync.dma_start(out, result[:])

@@ -48,13 +48,17 @@ def tile_moe_ser_none_kernel(
             return list_tile[:, first // PER_COLUMN : (first + count) // PER_COLUMN]
 
         xs = keep.tile([P, T], U8, name="xs", tag="xs_then_w1", align_bytes=64)
-        nc.gpsimd.memset(xs[:].bitcast(I32), 0)
+        nc.vector.memset(xs[:].bitcast(I32), 0)
         for s in range(PASSES):
             nc.sync.dma_start(xs[s : 16 * ROWS : ROWS, :].bitcast(I32), x_scales[s].bitcast(I32))
 
         gate_rows = keep.tile([P, P], F32, name="gate_rows")
-        nc.gpsimd.memset(gate_rows[:], 0.0)
+        nc.vector.memset(gate_rows[:], 0.0)
         nc.scalar.dma_start(gate_rows[0:E1, :], gate1[0].rearrange("(e c) -> e c", e=E1))
+
+        ident = keep.tile([P, P], F32, name="ident")
+        nc.vector.memset(ident[:], 0.0)
+        make_identity(nc, ident[:], nomemset=True)
 
         x_first = keep.tile([P, T], I32, name="x_first")
         nc.sync.dma_start(x_first[:], x_words[0].rearrange("p t d -> p (t d)").bitcast(I32))
@@ -91,9 +95,6 @@ def tile_moe_ser_none_kernel(
         load_w1_words("w1_1")
         load_scales(nc.scalar, ws[0], w1_scales[0:2])
 
-        ident = keep.tile([P, P], F32, name="ident")
-        make_identity(nc, ident[:])
-
         def gather_scales(part, queue):
             first, count = parts[part]
             picked = keep.tile([P, count], U8, name="picked%d" % part, align_bytes=64)
@@ -103,7 +104,7 @@ def tile_moe_ser_none_kernel(
                 queue.dma_start(dst, picked[LIVE * ROWS * q : LIVE * ROWS * (q + 1), :].bitcast(I32))
 
         gather_scales(0, nc.scalar)
-        gate_bank = psum.tile([P, P], F32, name="gate_bank", tag="y")
+        gate_bank = psum.tile([P, P], F32, name="gate_bank", tag="y", bufs=E2)
         nc.tensor.transpose(gate_bank[:], gate_rows[:], ident[:])
         gate_cols = keep.tile([P, E1], F32, name="gate_cols")
         nc.scalar.activation(gate_cols[:], gate_bank[:, 0:E1], COPY)
@@ -172,24 +173,28 @@ def tile_moe_ser_none_kernel(
         nc.sync.dma_start(g2[:], gate2)
 
         result = keep.tile([P, T], F32, name="result")
-        ys = keep.tile([P, T], F32, name="ys")
+        ys_last = keep.tile([P, 2 * C2], F32, name="ys_last")
+        ys = {2: ys_last[:, :C2], 3: ys_last[:, C2:]}
         woven = []
+        pairs = [keep.tile([P, 2 * C2], U32, name="pairs%d" % f, tag="pairs%d" % (f % 2)) for f in range(E2)]
 
-        def gather_c(f):
-            pairs = ring.tile([P, 2, C2], U32, name="pairs")
-            for u in range(2):
-                nc.vector.tensor_copy(pairs[:, u, :], c_pairs[u][:].bitcast(U32).indirect(entries(list2, f * C2, C2)))
+        def gather_pairs(f, u):
+            nc.vector.tensor_copy(pairs[f][:, u * C2 : (u + 1) * C2], c_pairs[u][:].bitcast(U32).indirect(entries(list2, f * C2, C2)))
+
+        def weave(f):
             values = ring.tile([P, 4 * C2], BF16, name="values", bufs=E2, align_bytes=64)
             nc.scalar.copy(
-                values[:].bitcast(U32).rearrange("p (m u) -> p m u", u=2), pairs[:].rearrange("p u m -> p m u")
+                values[:].bitcast(U32).rearrange("p (m u) -> p m u", u=2), pairs[f][:].rearrange("p (u m) -> p m u", u=2)
             )
             woven.append(values)
+
+        banks = []
 
         def multiply(f):
             codes = ring.tile([P, C2], U32, name="codes", bufs=E2, align_bytes=64)
             scales = ring.tile([P, C2], U8, name="scales", bufs=E2, align_bytes=64)
             nc.vector.quantize_mx(out=codes[:].bitcast(FP8X4), scales=scales[:], in_=woven[f][:])
-            y = psum.tile([P, C2], F32, name="y", tag="y")
+            y = psum.tile([P, C2], F32, name="y", tag="y", bufs=E2)
             nc.tensor.matmul_mx(
                 out=y[:],
                 lhsT=w2[:, f, :].bitcast(FP4X4),
@@ -199,15 +204,33 @@ def tile_moe_ser_none_kernel(
                 start=True,
                 stop=True,
             )
-            nc.scalar.copy(ys[:, f * C2 : (f + 1) * C2], y[:])
+            banks.append(y)
 
-        gather_c(0)
-        for f in range(1, E2):
-            gather_c(f)
-            multiply(f - 1)
-        multiply(E2 - 1)
+        def empty(f):
+            if f < 2:
+                ys[f] = keep.tile([P, C2], F32, name="ys%d" % f, tag="pairs1" if f == 1 else "ys0")[:]
+            nc.scalar.copy(ys[f], banks[f][:])
+
+        def scatter_y(f, experts):
+            first, count = f * C2, experts * C2
+            values = ys[f] if experts == 1 else ys_last[:]
+            nc.vector.tensor_tensor(
+                result[:].indirect(entries(list2, first, count)), values, g2[:, first : first + count], MULT
+            )
+
         for f in range(E2):
-            slots = slice(f * C2, (f + 1) * C2)
-            nc.vector.tensor_tensor(result[:].indirect(entries(list2, f * C2, C2)), ys[:, slots], g2[:, slots], MULT)
+            gather_pairs(f, 0)
+            gather_pairs(f, 1)
+            weave(f)
+            if f > 0:
+                multiply(f - 1)
+        empty(0)
+        scatter_y(0, 1)
+        multiply(E2 - 1)
+        empty(1)
+        scatter_y(1, 1)
+        empty(2)
+        empty(3)
+        scatter_y(2, 2)
 
         nc.sync.dma_start(out, result[:])

@@ -50,7 +50,7 @@ def tile_moe_ser_none_kernel(
         xs = keep.tile([P, T], U8, name="xs", tag="xs_then_w1", align_bytes=64)
         nc.vector.memset(xs[:].bitcast(I32), 0)
         for s in range(PASSES):
-            nc.sync.dma_start(xs[s : 16 * ROWS : ROWS, :].bitcast(I32), x_scales[s].bitcast(I32))
+            (nc.scalar if s else nc.sync).dma_start(xs[s : 16 * ROWS : ROWS, :].bitcast(I32), x_scales[s].bitcast(I32))
 
         gate_rows = keep.tile([P, P], F32, name="gate_rows")
         nc.vector.memset(gate_rows[:], 0.0)
@@ -76,12 +76,12 @@ def tile_moe_ser_none_kernel(
         for planes in ws[1:]:
             nc.vector.memset(planes[:].bitcast(I32), 0)
 
-        def load_scales(queue, planes, src):
+        def load_scales(queues, planes, src):
             rows = src.rearrange("e s (q r) i -> r q (e s) i", r=LIVE)
             width = rows.shape[2] * rows.shape[3]
             for r in range(LIVE):
                 dst = planes[r:P:QUADRANT, :width].bitcast(I32).rearrange("q (g i) -> q g i", g=rows.shape[2])
-                queue.dma_start(dst, rows[r].bitcast(I32))
+                queues[r].dma_start(dst, rows[r].bitcast(I32))
 
         w1 = []
 
@@ -89,15 +89,21 @@ def tile_moe_ser_none_kernel(
             e = len(w1)
             words = keep.tile([P, PASSES, 2 * H], U8, name="w1_%d" % e, tag=tag, align_bytes=64)
             nc.sync.dma_start(words[:].bitcast(I32), w1_words[e].rearrange("s p b -> p s b").bitcast(I32))
-            w1.append(words)
+            w1.append(words[:])
 
-        load_w1_words("w1_0")
-        load_w1_words("w1_1")
-        load_scales(nc.scalar, ws[0], w1_scales[0:2])
+        first_words = keep.tile([P, 2, PASSES, 2 * H], U8, name="w1_first", align_bytes=64)
+        nc.sync.dma_start(
+            first_words[:].bitcast(I32).rearrange("p e s b -> p (e s) b"),
+            w1_words[0:2].rearrange("e s p b -> p (e s) b").bitcast(I32),
+        )
+        w1.extend([first_words[:, 0], first_words[:, 1]])
+        load_scales([nc.scalar, nc.scalar, nc.sync, nc.sync], ws[0], w1_scales[0:2])
+
+        load_w1_words("w1_2")
 
         def gather_scales(part, queue):
             first, count = parts[part]
-            picked = keep.tile([P, count], U8, name="picked%d" % part, align_bytes=64)
+            picked = keep.tile([P, count], U8, name="picked%d" % part, tag="picked%d" % part, align_bytes=64)
             nc.vector.tensor_copy(picked[:], xs[:].indirect(entries(list1, first, count)))
             for q in range(P // QUADRANT):
                 dst = xp[part][QUADRANT * q : QUADRANT * q + LIVE, :, :].bitcast(I32)
@@ -111,14 +117,15 @@ def tile_moe_ser_none_kernel(
         gather_scales(1, nc.sync)
 
         for couple in range(1, COUPLES):
-            load_w1_words("xs_then_w1" if couple == 1 else "w1_%d" % (2 * couple))
+            if couple > 1:
+                load_w1_words("w1_%d" % (2 * couple))
+            load_w1_words("xs_then_w1" if couple == 1 else "w1_%d" % (2 * couple + 1))
             if couple < SCALE_TILES:
-                load_scales(nc.sync, ws[couple], w1_scales[2 * couple : 2 * couple + 2])
-            load_w1_words("w1_%d" % (2 * couple + 1))
+                load_scales([nc.sync] * LIVE, ws[couple], w1_scales[2 * couple : 2 * couple + 2])
 
         xg = {}
         for first in range(0, T, T // 2):
-            words = keep.tile([P, T // 2], U32, name="xg_first%d" % first, align_bytes=64)
+            words = keep.tile([P, T // 2], U32, name="xg_first%d" % first, tag="picked0" if first else "xg_first", align_bytes=64)
             nc.vector.tensor_copy(words[:], x_first[:].bitcast(U32).indirect(entries(list1, first, T // 2)))
             for j in range(E1 // 2):
                 xg[(first // C1 + j, 0)] = words[:, j * C1 : (j + 1) * C1]
@@ -129,6 +136,7 @@ def tile_moe_ser_none_kernel(
                 nc.vector.tensor_copy(words[:], x_rest[:, s - 1, :].bitcast(U32).indirect(offsets))
                 for j in range(2):
                     xg[(2 * couple + j, s)] = words[:, j * C1 : (j + 1) * C1]
+
 
         c_pairs = [keep.tile([P, T], F32, name="c_pairs%d" % u) for u in range(2)]
         for e in range(E1):
@@ -148,7 +156,7 @@ def tile_moe_ser_none_kernel(
                     stop=(s == PASSES - 1),
                 )
             if e == 1:
-                load_scales(nc.sync, ws[0], w1_scales[E1 - 2 : E1])
+                load_scales([nc.sync] * LIVE, ws[0], w1_scales[E1 - 2 : E1])
 
             gated = ring.tile([P, H], BF16, name="gated", bufs=E1 // 2)
             nc.scalar.activation(
@@ -168,7 +176,7 @@ def tile_moe_ser_none_kernel(
         nc.sync.dma_start(list2[:], offs2)
         w2 = keep.tile([P, E2, 2 * N], U8, name="w2", align_bytes=64)
         nc.sync.dma_start(w2[:].bitcast(I32), w2_words[:, 0].rearrange("f p b -> p f b").bitcast(I32))
-        load_scales(nc.sync, ws[1], w2_scales)
+        load_scales([nc.sync] * LIVE, ws[1], w2_scales)
         g2 = keep.tile([P, T], F32, name="g2", tag="x_rest_then_gate2")
         nc.sync.dma_start(g2[:], gate2)
 

@@ -27,6 +27,7 @@ PER_COLUMN = 16
 ROWS = 4
 COUPLES = E1 // 2
 COUPLE_SLOTS = 2 * C1
+PIECE = 128
 SCALE_TILES = 3
 
 
@@ -62,7 +63,7 @@ def tile_moe_ser_none_kernel(
 
         x_first = keep.tile([P, T], I32, name="x_first")
         nc.sync.dma_start(x_first[:], x_words[0].rearrange("p t d -> p (t d)").bitcast(I32))
-        x_rest = keep.tile([P, PASSES - 1, T], I32, name="x_rest", tag="x_rest_then_gate2")
+        x_rest = keep.tile([P, PASSES - 1, T], I32, name="x_rest", tag="x_rest_then_gate2", align_bytes=64)
         nc.sync.dma_start(x_rest[:], x_words[1:].rearrange("s p t d -> p s (t d)").bitcast(I32))
 
         ws = []
@@ -177,32 +178,44 @@ def tile_moe_ser_none_kernel(
         w2 = keep.tile([P, E2, 2 * N], U8, name="w2", align_bytes=64)
         nc.sync.dma_start(w2[:].bitcast(I32), w2_words[:, 0].rearrange("f p b -> p f b").bitcast(I32))
         load_scales([nc.sync] * LIVE, ws[1], w2_scales)
-        g2 = keep.tile([P, T], F32, name="g2", tag="x_rest_then_gate2")
-        nc.sync.dma_start(g2[:], gate2)
+        stage = keep.tile([P, 5 * T], F32, name="stage", tag="x_rest_then_gate2", align_bytes=64)
+        gates_at, values_at = 5 * PIECE, 5 * PIECE + T
+        nc.sync.dma_start(stage[:, gates_at : gates_at + T], gate2)
 
         result = keep.tile([P, T], F32, name="result")
-        ys_last = keep.tile([P, 2 * C2], F32, name="ys_last")
-        ys = {2: ys_last[:, :C2], 3: ys_last[:, C2:]}
-        woven = []
-        pairs = [keep.tile([P, 2 * C2], U32, name="pairs%d" % f, tag="pairs%d" % (f % 2)) for f in range(E2)]
+        pieces = T // PIECE
+        banks = {}
 
-        def gather_pairs(f, u):
-            nc.vector.tensor_copy(pairs[f][:, u * C2 : (u + 1) * C2], c_pairs[u][:].bitcast(U32).indirect(entries(list2, f * C2, C2)))
+        def gates(c):
+            return stage[:, gates_at + c * PIECE : gates_at + (c + 1) * PIECE]
 
-        def weave(f):
-            values = ring.tile([P, 4 * C2], BF16, name="values", bufs=E2, align_bytes=64)
-            nc.scalar.copy(
-                values[:].bitcast(U32).rearrange("p (m u) -> p m u", u=2), pairs[f][:].rearrange("p (u m) -> p m u", u=2)
-            )
-            woven.append(values)
+        def values(c):
+            return stage[:, values_at + 2 * c * PIECE : values_at + 2 * (c + 1) * PIECE]
 
-        banks = []
+        def pair_places(c):
+            place0 = gates_at + (c - 3) * PIECE if c >= 3 else 2 * c * PIECE
+            place1 = values_at + 2 * (c - 2) * PIECE if c >= 2 else (2 * c + 1) * PIECE
+            return place0, place1
 
-        def multiply(f):
-            codes = ring.tile([P, C2], U32, name="codes", bufs=E2, align_bytes=64)
-            scales = ring.tile([P, C2], U8, name="scales", bufs=E2, align_bytes=64)
-            nc.vector.quantize_mx(out=codes[:].bitcast(FP8X4), scales=scales[:], in_=woven[f][:])
-            y = psum.tile([P, C2], F32, name="y", tag="y", bufs=E2)
+        def gather_pairs(c):
+            for u in (1, 0) if c >= 3 else (0, 1):
+                at = pair_places(c)[u]
+                nc.vector.tensor_copy(
+                    stage[:, at : at + PIECE].bitcast(U32), c_pairs[u][:].bitcast(U32).indirect(entries(list2, c * PIECE, PIECE))
+                )
+
+        def weave(c):
+            place0, place1 = pair_places(c)
+            both = stage[:, place0 : 2 * place1 - place0].bitcast(U32).rearrange("p (u m) -> p m u", u=2)
+            copy = nc.scalar.copy if c < 3 else nc.vector.tensor_copy
+            copy(values(c).bitcast(U32).rearrange("p (m u) -> p m u", u=2), both[:, :PIECE, :])
+
+        def multiply(c):
+            f = c * PIECE // C2
+            codes = ring.tile([P, PIECE], U32, name="codes", bufs=pieces, align_bytes=64)
+            scales = ring.tile([P, PIECE], U8, name="scales", bufs=pieces, align_bytes=64)
+            nc.vector.quantize_mx(out=codes[:].bitcast(FP8X4), scales=scales[:], in_=values(c).bitcast(BF16))
+            y = psum.tile([P, PIECE], F32, name="y", tag="y", bufs=E2)
             nc.tensor.matmul_mx(
                 out=y[:],
                 lhsT=w2[:, f, :].bitcast(FP4X4),
@@ -212,33 +225,26 @@ def tile_moe_ser_none_kernel(
                 start=True,
                 stop=True,
             )
-            banks.append(y)
+            banks[c] = y
 
-        def empty(f):
-            if f < 2:
-                ys[f] = keep.tile([P, C2], F32, name="ys%d" % f, tag="pairs1" if f == 1 else "ys0")[:]
-            nc.scalar.copy(ys[f], banks[f][:])
+        def finish(c):
+            gated_y = ring.tile([P, PIECE], F32, name="gated_y", bufs=pieces)
+            nc.vector.tensor_tensor(gated_y[:], banks[c][:], gates(c), MULT)
+            return gated_y
 
-        def scatter_y(f, experts):
-            first, count = f * C2, experts * C2
-            values = ys[f] if experts == 1 else ys_last[:]
-            nc.vector.tensor_tensor(
-                result[:].indirect(entries(list2, first, count)), values, g2[:, first : first + count], MULT
-            )
+        def scatter(c, gated_y):
+            nc.scalar.activation(result[:].indirect(entries(list2, c * PIECE, PIECE)), gated_y[:], COPY)
 
-        for f in range(E2):
-            gather_pairs(f, 0)
-            gather_pairs(f, 1)
-            weave(f)
-            if f > 0:
-                multiply(f - 1)
-        empty(0)
-        scatter_y(0, 1)
-        multiply(E2 - 1)
-        empty(1)
-        scatter_y(1, 1)
-        empty(2)
-        empty(3)
-        scatter_y(2, 2)
+        for c in range(pieces + 3):
+            if 2 <= c < pieces + 2:
+                multiply(c - 2)
+            if c >= 3:
+                scatter(c - 3, finish(c - 3))
+            if 3 < c <= pieces:
+                weave(c - 1)
+            if c < pieces:
+                gather_pairs(c)
+            if c < 3:
+                weave(c)
 
         nc.sync.dma_start(out, result[:])

@@ -130,14 +130,12 @@ def tile_moe_ser_none_kernel(
             nc.vector.tensor_copy(words[:], x_first[:].bitcast(U32).indirect(entries(list1, first, T // 2)))
             for j in range(E1 // 2):
                 xg[(first // C1 + j, 0)] = words[:, j * C1 : (j + 1) * C1]
-        for couple in range(COUPLES):
-            offsets = entries(list1, couple * COUPLE_SLOTS, COUPLE_SLOTS)
+        for first, count in parts:
             for s in range(1, PASSES):
-                words = keep.tile([P, COUPLE_SLOTS], U32, name="xg%d_%d" % (couple, s), align_bytes=64)
-                nc.vector.tensor_copy(words[:], x_rest[:, s - 1, :].bitcast(U32).indirect(offsets))
-                for j in range(2):
-                    xg[(2 * couple + j, s)] = words[:, j * C1 : (j + 1) * C1]
-
+                words = keep.tile([P, count], U32, name="xg%d_%d" % (first, s), align_bytes=64)
+                nc.vector.tensor_copy(words[:], x_rest[:, s - 1, :].bitcast(U32).indirect(entries(list1, first, count)))
+                for j in range(count // C1):
+                    xg[(first // C1 + j, s)] = words[:, j * C1 : (j + 1) * C1]
 
         c_pairs = [keep.tile([P, T], F32, name="c_pairs%d" % u) for u in range(2)]
         for e in range(E1):

@@ -28,7 +28,7 @@ ROWS = 4
 COUPLES = E1 // 2
 COUPLE_SLOTS = 2 * C1
 PIECE = 128
-SCALE_TILES = 3
+SCALE_TILES = 2
 
 
 def tile_moe_ser_none_kernel(
@@ -117,7 +117,7 @@ def tile_moe_ser_none_kernel(
         nc.scalar.activation(gate_cols[:], gate_bank[:, 0:E1], COPY)
         gather_scales(1, nc.sync)
 
-        for couple in range(1, COUPLES):
+        for couple in range(1, COUPLES - 1):
             if couple > 1:
                 load_w1_words("w1_%d" % (2 * couple))
             load_w1_words("xs_then_w1" if couple == 1 else "w1_%d" % (2 * couple + 1))
@@ -154,8 +154,11 @@ def tile_moe_ser_none_kernel(
                     start=(s == 0),
                     stop=(s == PASSES - 1),
                 )
+            if j == 1 and couple + SCALE_TILES < COUPLES:
+                load_scales([nc.sync] * LIVE, ws[couple], w1_scales[e + 3 : e + 5])
             if e == 1:
-                load_scales([nc.sync] * LIVE, ws[0], w1_scales[E1 - 2 : E1])
+                load_w1_words("w1_6")
+                load_w1_words("w1_7")
 
             gated = ring.tile([P, H], BF16, name="gated", bufs=E1 // 2)
             nc.scalar.activation(
@@ -175,7 +178,7 @@ def tile_moe_ser_none_kernel(
         nc.sync.dma_start(list2[:], offs2)
         w2 = keep.tile([P, E2, 2 * N], U8, name="w2", align_bytes=64)
         nc.sync.dma_start(w2[:].bitcast(I32), w2_words[:, 0].rearrange("f p b -> p f b").bitcast(I32))
-        load_scales([nc.sync] * LIVE, ws[1], w2_scales)
+        load_scales([nc.sync] * LIVE, ws[0], w2_scales)
         stage = keep.tile([P, 5 * T], F32, name="stage", tag="x_rest_then_gate2", align_bytes=64)
         gates_at, values_at = 5 * PIECE, 5 * PIECE + T
         nc.sync.dma_start(stage[:, gates_at : gates_at + T], gate2)
@@ -217,7 +220,7 @@ def tile_moe_ser_none_kernel(
             nc.tensor.matmul_mx(
                 out=y[:],
                 lhsT=w2[:, f, :].bitcast(FP4X4),
-                lhsT_scale=ws[1][:, f * N : (f + 1) * N],
+                lhsT_scale=ws[0][:, f * N : (f + 1) * N],
                 rhs=codes[:].bitcast(FP8X4),
                 rhs_scale=scales[:],
                 start=True,

@@ -18,17 +18,15 @@ FP8X4 = mybir.dt.float8_e4m3fn_x4
 FP4X4 = mybir.dt.float4_e2m1fn_x4
 COPY = mybir.ActivationFunctionType.Copy
 MULT = mybir.AluOpType.mult
+ADD = mybir.AluOpType.add
 
 P = 128
 PASSES = K // 512
 QUADRANT = 32
 LIVE = 4
 PER_COLUMN = 16
-ROWS = 4
-COUPLES = E1 // 2
-COUPLE_SLOTS = 2 * C1
-PIECE = 128
-SCALE_TILES = 2
+RUNS = ((0, 2), (2, 5), (5, 8))
+PIECES = ((0, 128), (128, 128), (256, 128), (384, 256), (640, 256), (896, 128))
 
 
 def tile_moe_ser_none_kernel(
@@ -38,7 +36,6 @@ def tile_moe_ser_none_kernel(
     with ExitStack() as ctx:
         lists = ctx.enter_context(tc.tile_pool(name="lists", bufs=1))
         keep = ctx.enter_context(tc.tile_pool(name="keep", bufs=1))
-        ring = ctx.enter_context(tc.tile_pool(name="ring", bufs=2))
         psum = ctx.enter_context(tc.psum_pool(name="psum", bufs=2))
 
         list1 = lists.tile([P, T // PER_COLUMN], U16, name="list1")
@@ -48,119 +45,106 @@ def tile_moe_ser_none_kernel(
         def entries(list_tile, first, count):
             return list_tile[:, first // PER_COLUMN : (first + count) // PER_COLUMN]
 
-        xs = keep.tile([P, T], U8, name="xs", tag="xs_then_w1", align_bytes=64)
+        xs = keep.tile([P, T], U8, name="xs", tag="xs_then_words", align_bytes=64)
         nc.vector.memset(xs[:].bitcast(I32), 0)
-        for s in range(PASSES):
-            (nc.scalar if s else nc.sync).dma_start(xs[s : 16 * ROWS : ROWS, :].bitcast(I32), x_scales[s].bitcast(I32))
+        zero = keep.tile([P, 8], I32, name="zero")
+        nc.vector.memset(zero[:], 0)
+        x_first = keep.tile([P, T], I32, name="x_first")
+        nc.sync.dma_start(x_first[:], x_words[0].rearrange("p t d -> p (t d)").bitcast(I32))
+        for q in range(4):
+            dst = xs[QUADRANT * q : QUADRANT * q + LIVE, :].bitcast(I32)
+            nc.scalar.dma_start(dst, x_scales[0, LIVE * q : LIVE * (q + 1), :].bitcast(I32))
+        for half in range(2):
+            at = LIVE + 64 * half
+            src = x_scales[1:3, 8 * half : 8 * half + 8, :].rearrange("s b t -> b s t")
+            nc.sync.dma_start(xs[at : at + 16, :].bitcast(I32), src.bitcast(I32))
+        x_rest = keep.tile([P, PASSES - 1, T], I32, name="x_rest")
+        nc.sync.dma_start(x_rest[:], x_words[1:].rearrange("s p t d -> p s (t d)").bitcast(I32))
+        x = [x_first[:], x_rest[:, 0, :], x_rest[:, 1, :]]
 
+        slot = PASSES * H
+        ws = [keep.tile([P, 3 * slot], U8, name="ws%d" % i, align_bytes=64) for i in range(2)]
+        nc.vector.memset(ws[0][:, : 2 * slot].bitcast(I32), 0)
         gate_rows = keep.tile([P, P], F32, name="gate_rows")
         nc.vector.memset(gate_rows[:], 0.0)
-        nc.scalar.dma_start(gate_rows[0:E1, :], gate1[0].rearrange("(e c) -> e c", e=E1))
-
         ident = keep.tile([P, P], F32, name="ident")
         nc.vector.memset(ident[:], 0.0)
         make_identity(nc, ident[:], nomemset=True)
+        xp = keep.tile([P, 2, T], U8, name="xp", align_bytes=64)
+        nc.vector.memset(xp[:].bitcast(I32), 0)
 
-        x_first = keep.tile([P, T], I32, name="x_first")
-        nc.sync.dma_start(x_first[:], x_words[0].rearrange("p t d -> p (t d)").bitcast(I32))
-        x_rest = keep.tile([P, PASSES - 1, T], I32, name="x_rest", tag="x_rest_then_gate2", align_bytes=64)
-        nc.sync.dma_start(x_rest[:], x_words[1:].rearrange("s p t d -> p s (t d)").bitcast(I32))
+        def clear(region):
+            words = region.bitcast(U32)
+            nc.scalar.copy(words, zero[:, 0:1].bitcast(U32).to_broadcast(list(words.shape)))
 
-        ws = []
-        for i in range(SCALE_TILES):
-            ws.append(keep.tile([P, 2 * PASSES * H], U8, name="ws%d" % i, align_bytes=64))
-        parts = ((0, COUPLE_SLOTS), (COUPLE_SLOTS, T - COUPLE_SLOTS))
-        xp = [keep.tile([P, ROWS, count], U8, name="xp%d" % first, align_bytes=64) for first, count in parts]
-        nc.vector.memset(ws[0][:].bitcast(I32), 0)
-        for planes in xp:
-            nc.vector.memset(planes[:, :PASSES, :].bitcast(I32), 0)
-        for planes in ws[1:]:
-            nc.vector.memset(planes[:].bitcast(I32), 0)
+        windows = [keep.tile([P, T], F32, name="window%d" % i) for i in range(2)]
+        clear(ws[1][:])
+        clear(ws[0][:, 2 * slot :])
+        for window in windows:
+            nc.scalar.copy(window[:], zero[:, 0:1].bitcast(F32).to_broadcast([P, T]))
 
-        def load_scales(queues, planes, src):
+        def load_scales(planes, src):
             rows = src.rearrange("e s (q r) i -> r q (e s) i", r=LIVE)
             width = rows.shape[2] * rows.shape[3]
             for r in range(LIVE):
                 dst = planes[r:P:QUADRANT, :width].bitcast(I32).rearrange("q (g i) -> q g i", g=rows.shape[2])
-                queues[r].dma_start(dst, rows[r].bitcast(I32))
+                nc.sync.dma_start(dst, rows[r].bitcast(I32))
 
-        w1 = []
+        w1 = [keep.tile([P, PASSES, 2 * H], U8, name="w1_%d" % e, align_bytes=64) for e in range(E1)]
 
-        def load_w1_words(tag):
-            e = len(w1)
-            words = keep.tile([P, PASSES, 2 * H], U8, name="w1_%d" % e, tag=tag, align_bytes=64)
-            nc.sync.dma_start(words[:].bitcast(I32), w1_words[e].rearrange("s p b -> p s b").bitcast(I32))
-            w1.append(words[:])
+        def load_w1(e):
+            nc.sync.dma_start(w1[e][:].bitcast(I32), w1_words[e].rearrange("s p b -> p s b").bitcast(I32))
 
-        first_words = keep.tile([P, 2, PASSES, 2 * H], U8, name="w1_first", align_bytes=64)
-        nc.sync.dma_start(
-            first_words[:].bitcast(I32).rearrange("p e s b -> p (e s) b"),
-            w1_words[0:2].rearrange("e s p b -> p (e s) b").bitcast(I32),
-        )
-        w1.extend([first_words[:, 0], first_words[:, 1]])
-        load_scales([nc.scalar, nc.scalar, nc.sync, nc.sync], ws[0], w1_scales[0:2])
+        load_w1(0)
+        load_scales(ws[0], w1_scales[0:2])
+        nc.sync.dma_start(gate_rows[0:E1, :], gate1[0].rearrange("(e c) -> e c", e=E1))
+        load_w1(1)
 
-        load_w1_words("w1_2")
+        picked = keep.tile([P, T], U8, name="picked", align_bytes=64)
+        for first in (0, T // 2):
+            nc.vector.tensor_copy(picked[:, first : first + T // 2], xs[:].indirect(entries(list1, first, T // 2)))
+        for q in range(4):
+            at = LIVE + 64 * (q // 2) + 8 * (q % 2)
+            nc.sync.dma_start(xp[QUADRANT * q : QUADRANT * q + LIVE, :, :].bitcast(I32), picked[at : at + 8, :].bitcast(I32))
+        load_scales(ws[1], w1_scales[2:5])
+        for e in range(2, 5):
+            load_w1(e)
 
-        def gather_scales(part, queue):
-            first, count = parts[part]
-            picked = keep.tile([P, count], U8, name="picked%d" % part, tag="picked%d" % part, align_bytes=64)
-            nc.vector.tensor_copy(picked[:], xs[:].indirect(entries(list1, first, count)))
-            for q in range(P // QUADRANT):
-                dst = xp[part][QUADRANT * q : QUADRANT * q + LIVE, :, :].bitcast(I32)
-                queue.dma_start(dst, picked[LIVE * ROWS * q : LIVE * ROWS * (q + 1), :].bitcast(I32))
-
-        gather_scales(0, nc.scalar)
-        gate_bank = psum.tile([P, P], F32, name="gate_bank", tag="y", bufs=E2)
+        gate_bank = psum.tile([P, P], F32, name="gate_bank", tag="y", bufs=3)
         nc.tensor.transpose(gate_bank[:], gate_rows[:], ident[:])
         gate_cols = keep.tile([P, E1], F32, name="gate_cols")
-        nc.scalar.activation(gate_cols[:], gate_bank[:, 0:E1], COPY)
-        gather_scales(1, nc.sync)
-
-        for couple in range(1, COUPLES - 1):
-            if couple > 1:
-                load_w1_words("w1_%d" % (2 * couple))
-            load_w1_words("xs_then_w1" if couple == 1 else "w1_%d" % (2 * couple + 1))
-            if couple < SCALE_TILES:
-                load_scales([nc.sync] * LIVE, ws[couple], w1_scales[2 * couple : 2 * couple + 2])
+        nc.scalar.copy(gate_cols[:], gate_bank[:, 0:E1])
 
         xg = {}
-        for first in range(0, T, T // 2):
-            words = keep.tile([P, T // 2], U32, name="xg_first%d" % first, tag="picked0" if first else "xg_first", align_bytes=64)
-            nc.vector.tensor_copy(words[:], x_first[:].bitcast(U32).indirect(entries(list1, first, T // 2)))
-            for j in range(E1 // 2):
-                xg[(first // C1 + j, 0)] = words[:, j * C1 : (j + 1) * C1]
-        for first, count in parts:
-            for s in range(1, PASSES):
-                words = keep.tile([P, count], U32, name="xg%d_%d" % (first, s), align_bytes=64)
-                nc.vector.tensor_copy(words[:], x_rest[:, s - 1, :].bitcast(U32).indirect(entries(list1, first, count)))
-                for j in range(count // C1):
-                    xg[(first // C1 + j, s)] = words[:, j * C1 : (j + 1) * C1]
+        for s, first, count in ((0, 0, 256), (1, 0, 256), (2, 0, 256), (0, 256, 768), (1, 256, 768), (2, 256, 768)):
+            tag = "xs_then_words" if (s, first) == (0, 256) else "xg%d_%d" % (s, first)
+            words = keep.tile([P, count], U32, name="xg%d_%d" % (s, first), tag=tag, align_bytes=64)
+            nc.vector.tensor_copy(words[:], x[s].bitcast(U32).indirect(entries(list1, first, count)))
+            for j in range(count // C1):
+                xg[(first // C1 + j, s)] = words[:, j * C1 : (j + 1) * C1]
 
         c_pairs = [keep.tile([P, T], F32, name="c_pairs%d" % u) for u in range(2)]
         for e in range(E1):
-            couple, j = divmod(e, 2)
-            part = min(couple, 1)
-            column = e * C1 - parts[part][0]
-            h = psum.tile([P, H], F32, name="h", tag="h")
+            run = [i for i in range(len(RUNS)) if RUNS[i][0] <= e < RUNS[i][1]][0]
+            place = e - RUNS[run][0]
+            columns = slice(e * C1, (e + 1) * C1)
+            h = psum.tile([P, H], F32, name="h", tag="h", bufs=3)
             for s in range(PASSES):
-                plane = j * PASSES + s
+                plane = place * PASSES + s
                 nc.tensor.matmul_mx(
                     out=h[:],
                     lhsT=xg[(e, s)].bitcast(FP8X4),
-                    lhsT_scale=xp[part][:, s, column : column + C1],
+                    lhsT_scale=xp[:, s - 1, columns] if s else picked[:, columns],
                     rhs=w1[e][:, s, :].bitcast(FP4X4),
-                    rhs_scale=ws[couple % SCALE_TILES][:, plane * H : (plane + 1) * H],
+                    rhs_scale=ws[run % 2][:, plane * H : (plane + 1) * H],
                     start=(s == 0),
                     stop=(s == PASSES - 1),
                 )
-            if j == 1 and couple + SCALE_TILES < COUPLES:
-                load_scales([nc.sync] * LIVE, ws[couple], w1_scales[e + 3 : e + 5])
             if e == 1:
-                load_w1_words("w1_6")
-                load_w1_words("w1_7")
-
-            gated = ring.tile([P, H], BF16, name="gated", bufs=E1 // 2)
+                load_scales(ws[0], w1_scales[5:8])
+                for later in range(5, 8):
+                    load_w1(later)
+            gated = keep.tile([P, H], BF16, name="gated", tag="gated%d" % e)
             nc.scalar.activation(
                 gated[:].rearrange("c (u p v) -> c u p v", u=2, v=2),
                 h[:].rearrange("c (p u v) -> c u p v", u=2, v=2),
@@ -170,7 +154,7 @@ def tile_moe_ser_none_kernel(
             turned = psum.tile([P, 2, C1], F32, name="turned", tag="turned")
             for u in range(2):
                 nc.tensor.transpose(turned[:, u, :], gated[:].bitcast(F32)[:, u * P : (u + 1) * P], ident[:])
-            staged = ring.tile([P, 2, C1], F32, name="staged", bufs=E1)
+            staged = keep.tile([P, 2, C1], F32, name="staged%d" % e)
             nc.scalar.copy(staged[:], turned[:])
             for u in range(2):
                 nc.vector.tensor_copy(c_pairs[u][:].indirect(entries(list1, e * C1, C1)), staged[:, u, :])
@@ -178,74 +162,86 @@ def tile_moe_ser_none_kernel(
         nc.sync.dma_start(list2[:], offs2)
         w2 = keep.tile([P, E2, 2 * N], U8, name="w2", align_bytes=64)
         nc.sync.dma_start(w2[:].bitcast(I32), w2_words[:, 0].rearrange("f p b -> p f b").bitcast(I32))
-        load_scales([nc.sync] * LIVE, ws[0], w2_scales)
-        stage = keep.tile([P, 5 * T], F32, name="stage", tag="x_rest_then_gate2", align_bytes=64)
-        gates_at, values_at = 5 * PIECE, 5 * PIECE + T
-        nc.sync.dma_start(stage[:, gates_at : gates_at + T], gate2)
+        gates = keep.tile([P, T], F32, name="gates")
+        nc.sync.dma_start(gates[:], gate2)
+        load_scales(ws[1], w2_scales)
 
-        result = keep.tile([P, T], F32, name="result")
-        pieces = T // PIECE
-        banks = {}
+        products = keep.tile([P, T], F32, name="products")
+        pair_tags = ("pairs0", "pairs1", "pairs0", "scales0", "scales1", "scales0")
+        code_tags = ("codes0", "codes0", "codes0", "codes3", "codes4", "codes3")
+        values, banks = {}, {}
 
-        def gates(c):
-            return stage[:, gates_at + c * PIECE : gates_at + (c + 1) * PIECE]
+        def gather(c):
+            first, count = PIECES[c]
+            pairs = keep.tile([P, 2, count], U32, name="pairs%d" % c, tag=pair_tags[c], align_bytes=64)
+            for u in range(2):
+                nc.vector.tensor_copy(pairs[:, u, :], c_pairs[u][:].bitcast(U32).indirect(entries(list2, first, count)))
+            values[c] = keep.tile([P, count, 2], U32, name="values%d" % c, align_bytes=64)
+            nc.scalar.copy(values[c][:], pairs[:].rearrange("p u m -> p m u"))
 
-        def values(c):
-            return stage[:, values_at + 2 * c * PIECE : values_at + 2 * (c + 1) * PIECE]
-
-        def pair_places(c):
-            place0 = gates_at + (c - 3) * PIECE if c >= 3 else 2 * c * PIECE
-            place1 = values_at + 2 * (c - 2) * PIECE if c >= 2 else (2 * c + 1) * PIECE
-            return place0, place1
-
-        def gather_pairs(c):
-            for u in (1, 0) if c >= 3 else (0, 1):
-                at = pair_places(c)[u]
-                nc.vector.tensor_copy(
-                    stage[:, at : at + PIECE].bitcast(U32), c_pairs[u][:].bitcast(U32).indirect(entries(list2, c * PIECE, PIECE))
-                )
-
-        def weave(c):
-            place0, place1 = pair_places(c)
-            both = stage[:, place0 : 2 * place1 - place0].bitcast(U32).rearrange("p (u m) -> p m u", u=2)
-            copy = nc.scalar.copy if c < 3 else nc.vector.tensor_copy
-            copy(values(c).bitcast(U32).rearrange("p (m u) -> p m u", u=2), both[:, :PIECE, :])
+        def gather_woven(c):
+            first, count = PIECES[c]
+            values[c] = keep.tile([P, count, 2], U32, name="values%d" % c, tag=pair_tags[c], align_bytes=64)
+            for u in range(2):
+                nc.vector.tensor_copy(values[c][:, :, u], c_pairs[u][:].bitcast(U32).indirect(entries(list2, first, count)))
 
         def multiply(c):
-            f = c * PIECE // C2
-            codes = ring.tile([P, PIECE], U32, name="codes", bufs=pieces, align_bytes=64)
-            scales = ring.tile([P, PIECE], U8, name="scales", bufs=pieces, align_bytes=64)
-            nc.vector.quantize_mx(out=codes[:].bitcast(FP8X4), scales=scales[:], in_=values(c).bitcast(BF16))
-            y = psum.tile([P, PIECE], F32, name="y", tag="y", bufs=E2)
-            nc.tensor.matmul_mx(
-                out=y[:],
-                lhsT=w2[:, f, :].bitcast(FP4X4),
-                lhsT_scale=ws[0][:, f * N : (f + 1) * N],
-                rhs=codes[:].bitcast(FP8X4),
-                rhs_scale=scales[:],
-                start=True,
-                stop=True,
+            first, count = PIECES[c]
+            codes = keep.tile([P, count], U32, name="codes%d" % c, tag=code_tags[c], align_bytes=64)
+            scales = keep.tile([P, count], U8, name="scales%d" % c, tag="scales%d" % c, align_bytes=64)
+            nc.vector.quantize_mx(
+                out=codes[:].bitcast(FP8X4), scales=scales[:], in_=values[c][:].rearrange("p m u -> p (m u)").bitcast(BF16)
             )
-            banks[c] = y
+            banks[c] = psum.tile([P, count], F32, name="y", tag="y", bufs=3)
+            for at in range(0, count, P):
+                f = (first + at) // C2
+                nc.tensor.matmul_mx(
+                    out=banks[c][:, at : at + P],
+                    lhsT=w2[:, f, :].bitcast(FP4X4),
+                    lhsT_scale=ws[1][:, f * N : (f + 1) * N],
+                    rhs=codes[:, at : at + P].bitcast(FP8X4),
+                    rhs_scale=scales[:, at : at + P],
+                    start=True,
+                    stop=True,
+                )
 
-        def finish(c):
-            gated_y = ring.tile([P, PIECE], F32, name="gated_y", bufs=pieces)
-            nc.vector.tensor_tensor(gated_y[:], banks[c][:], gates(c), MULT)
-            return gated_y
+        def gate(c):
+            first, count = PIECES[c]
+            nc.vector.tensor_tensor(products[:, first : first + count], banks[c][:], gates[:, first : first + count], MULT)
 
-        def scatter(c, gated_y):
-            nc.scalar.activation(result[:].indirect(entries(list2, c * PIECE, PIECE)), gated_y[:], COPY)
+        def scatter_scalar(first, count):
+            nc.scalar.activation(windows[0][:].indirect(entries(list2, first, count)), products[:, first : first + count], COPY)
 
-        for c in range(pieces + 3):
-            if 2 <= c < pieces + 2:
-                multiply(c - 2)
-            if c >= 3:
-                scatter(c - 3, finish(c - 3))
-            if 3 < c <= pieces:
-                weave(c - 1)
-            if c < pieces:
-                gather_pairs(c)
-            if c < 3:
-                weave(c)
+        def scatter_vector(first, count):
+            nc.vector.tensor_copy(windows[1][:].indirect(entries(list2, first, count)), products[:, first : first + count])
 
-        nc.sync.dma_start(out, result[:])
+        gather_woven(0)
+        multiply(0)
+        gather(1)
+        gather(2)
+        gate(0)
+        scatter_scalar(*PIECES[0])
+        multiply(1)
+        gather(3)
+        gate(1)
+        scatter_scalar(*PIECES[1])
+        multiply(2)
+        gather(4)
+        gate(2)
+        scatter_scalar(*PIECES[2])
+        multiply(3)
+        gather_woven(5)
+        multiply(4)
+        gate(3)
+        scatter_scalar(*PIECES[3])
+        multiply(5)
+        gate(4)
+        gate(5)
+        scatter_vector(*PIECES[4])
+        scatter_scalar(*PIECES[5])
+
+        result = keep.tile([P, T], F32, name="result")
+        for first in range(0, T, T // 2):
+            part = slice(first, first + T // 2)
+            nc.vector.tensor_tensor(result[:, part], windows[0][:, part], windows[1][:, part], ADD)
+            nc.sync.dma_start(out[:, part], result[:, part])

@@ -25,7 +25,7 @@ PASSES = K // 512
 QUADRANT = 32
 LIVE = 4
 PER_COLUMN = 16
-RUNS = ((0, 2), (2, 5), (5, 8))
+RUNS = ((0, 3), (3, 6), (6, 8))
 PIECES = ((0, 128), (128, 128), (256, 128), (384, 256), (640, 256), (896, 128))
 
 
@@ -45,7 +45,7 @@ def tile_moe_ser_none_kernel(
         def entries(list_tile, first, count):
             return list_tile[:, first // PER_COLUMN : (first + count) // PER_COLUMN]
 
-        xs = keep.tile([P, T], U8, name="xs", tag="xs_then_words", align_bytes=64)
+        xs = keep.tile([P, T], U8, name="xs", align_bytes=64)
         nc.vector.memset(xs[:].bitcast(I32), 0)
         zero = keep.tile([P, 8], I32, name="zero")
         nc.vector.memset(zero[:], 0)
@@ -64,8 +64,8 @@ def tile_moe_ser_none_kernel(
 
         slot = PASSES * H
         ws = [keep.tile([P, 3 * slot], U8, name="ws%d" % i, align_bytes=64) for i in range(2)]
-        nc.vector.memset(ws[0][:, : 2 * slot].bitcast(I32), 0)
-        gate_rows = keep.tile([P, P], F32, name="gate_rows")
+        nc.vector.memset(ws[0][:].bitcast(I32), 0)
+        gate_rows = keep.tile([P, P], F32, name="gate_rows", tag="gate_rows_then_words", align_bytes=64)
         nc.vector.memset(gate_rows[:], 0.0)
         ident = keep.tile([P, P], F32, name="ident")
         nc.vector.memset(ident[:], 0.0)
@@ -79,7 +79,6 @@ def tile_moe_ser_none_kernel(
 
         windows = [keep.tile([P, T], F32, name="window%d" % i) for i in range(2)]
         clear(ws[1][:])
-        clear(ws[0][:, 2 * slot :])
         for window in windows:
             nc.scalar.copy(window[:], zero[:, 0:1].bitcast(F32).to_broadcast([P, T]))
 
@@ -96,9 +95,8 @@ def tile_moe_ser_none_kernel(
             nc.sync.dma_start(w1[e][:].bitcast(I32), w1_words[e].rearrange("s p b -> p s b").bitcast(I32))
 
         load_w1(0)
-        load_scales(ws[0], w1_scales[0:2])
+        load_scales(ws[0], w1_scales[0:3])
         nc.sync.dma_start(gate_rows[0:E1, :], gate1[0].rearrange("(e c) -> e c", e=E1))
-        load_w1(1)
 
         picked = keep.tile([P, T], U8, name="picked", align_bytes=64)
         for first in (0, T // 2):
@@ -106,8 +104,10 @@ def tile_moe_ser_none_kernel(
         for q in range(4):
             at = LIVE + 64 * (q // 2) + 8 * (q % 2)
             nc.sync.dma_start(xp[QUADRANT * q : QUADRANT * q + LIVE, :, :].bitcast(I32), picked[at : at + 8, :].bitcast(I32))
-        load_scales(ws[1], w1_scales[2:5])
-        for e in range(2, 5):
+        load_w1(1)
+        load_w1(2)
+        load_scales(ws[1], w1_scales[3:6])
+        for e in range(3, 6):
             load_w1(e)
 
         gate_bank = psum.tile([P, P], F32, name="gate_bank", tag="y", bufs=3)
@@ -116,8 +116,8 @@ def tile_moe_ser_none_kernel(
         nc.scalar.copy(gate_cols[:], gate_bank[:, 0:E1])
 
         xg = {}
-        for s, first, count in ((0, 0, 256), (1, 0, 256), (2, 0, 256), (0, 256, 768), (1, 256, 768), (2, 256, 768)):
-            tag = "xs_then_words" if (s, first) == (0, 256) else "xg%d_%d" % (s, first)
+        for s, first, count in ((0, 0, 384), (1, 0, 384), (2, 0, 384), (1, 384, 640), (2, 384, 640), (0, 384, 640)):
+            tag = "gate_rows_then_words" if (s, first) == (0, 384) else "xg%d_%d" % (s, first)
             words = keep.tile([P, count], U32, name="xg%d_%d" % (s, first), tag=tag, align_bytes=64)
             nc.vector.tensor_copy(words[:], x[s].bitcast(U32).indirect(entries(list1, first, count)))
             for j in range(count // C1):
@@ -140,24 +140,24 @@ def tile_moe_ser_none_kernel(
                     start=(s == 0),
                     stop=(s == PASSES - 1),
                 )
-            if e == 1:
-                load_scales(ws[0], w1_scales[5:8])
-                for later in range(5, 8):
+            if e == 2:
+                load_scales(ws[0], w1_scales[6:8])
+                for later in range(6, 8):
                     load_w1(later)
-            gated = keep.tile([P, H], BF16, name="gated", tag="gated%d" % e)
-            nc.scalar.activation(
-                gated[:].rearrange("c (u p v) -> c u p v", u=2, v=2),
-                h[:].rearrange("c (p u v) -> c u p v", u=2, v=2),
-                COPY,
-                scale=gate_cols[:, e : e + 1],
-            )
-            turned = psum.tile([P, 2, C1], F32, name="turned", tag="turned")
-            for u in range(2):
-                nc.tensor.transpose(turned[:, u, :], gated[:].bitcast(F32)[:, u * P : (u + 1) * P], ident[:])
-            staged = keep.tile([P, 2, C1], F32, name="staged%d" % e)
-            nc.scalar.copy(staged[:], turned[:])
-            for u in range(2):
-                nc.vector.tensor_copy(c_pairs[u][:].indirect(entries(list1, e * C1, C1)), staged[:, u, :])
+            for planes in ((0,), (1,)) if e == 0 else ((0, 1),):
+                count = len(planes)
+                tag = "gated%d_%d" % (e, planes[0])
+                gated = keep.tile([P, count, P, 2], BF16, name="gated", tag=tag)
+                h_view = h[:].rearrange("c (p u v) -> c u p v", u=2, v=2)
+                nc.scalar.activation(gated[:], h_view[:, planes[0] : planes[-1] + 1], COPY, scale=gate_cols[:, e : e + 1])
+                words = gated[:].rearrange("c u p v -> c (u p v)").bitcast(F32)
+                turned = psum.tile([P, count, C1], F32, name="turned", tag="turned")
+                for j in range(count):
+                    nc.tensor.transpose(turned[:, j, :], words[:, j * P : (j + 1) * P], ident[:])
+                staged = keep.tile([P, count, C1], F32, name="staged%d_%d" % (e, planes[0]))
+                nc.scalar.copy(staged[:], turned[:])
+                for j in range(count):
+                    nc.vector.tensor_copy(c_pairs[planes[j]][:].indirect(entries(list1, e * C1, C1)), staged[:, j, :])
 
         nc.sync.dma_start(list2[:], offs2)
         w2 = keep.tile([P, E2, 2 * N], U8, name="w2", align_bytes=64)
@@ -241,7 +241,7 @@ def tile_moe_ser_none_kernel(
         scatter_scalar(*PIECES[5])
 
         result = keep.tile([P, T], F32, name="result")
-        for first in range(0, T, T // 2):
-            part = slice(first, first + T // 2)
+        for first in range(0, T, T // 4):
+            part = slice(first, first + T // 4)
             nc.vector.tensor_tensor(result[:, part], windows[0][:, part], windows[1][:, part], ADD)
             nc.sync.dma_start(out[:, part], result[:, part])

@@ -25,7 +25,7 @@ PASSES = K // 512
 QUADRANT = 32
 LIVE = 4
 PER_COLUMN = 16
-RUNS = ((0, 3), (3, 6), (6, 8))
+RUNS = ((0, 3), (3, 5), (5, 8))
 PIECES = ((0, 128), (128, 128), (256, 128), (384, 256), (640, 256), (896, 128))
 
 
@@ -47,7 +47,7 @@ def tile_moe_ser_none_kernel(
 
         xs = keep.tile([P, T], U8, name="xs", align_bytes=64)
         nc.vector.memset(xs[:].bitcast(I32), 0)
-        zero = keep.tile([P, 8], I32, name="zero")
+        zero = keep.tile([P, 8], I32, name="zero", tag="zero_then_words", align_bytes=64)
         nc.vector.memset(zero[:], 0)
         x_first = keep.tile([P, T], I32, name="x_first")
         nc.sync.dma_start(x_first[:], x_words[0].rearrange("p t d -> p (t d)").bitcast(I32))
@@ -63,7 +63,7 @@ def tile_moe_ser_none_kernel(
         x = [x_first[:], x_rest[:, 0, :], x_rest[:, 1, :]]
 
         slot = PASSES * H
-        ws = [keep.tile([P, 3 * slot], U8, name="ws%d" % i, align_bytes=64) for i in range(2)]
+        ws = [keep.tile([P, (3 - i) * slot], U8, name="ws%d" % i, align_bytes=64) for i in range(2)]
         nc.vector.memset(ws[0][:].bitcast(I32), 0)
         gate_rows = keep.tile([P, P], F32, name="gate_rows", tag="gate_rows_then_words", align_bytes=64)
         nc.vector.memset(gate_rows[:], 0.0)
@@ -89,25 +89,30 @@ def tile_moe_ser_none_kernel(
                 dst = planes[r:P:QUADRANT, :width].bitcast(I32).rearrange("q (g i) -> q g i", g=rows.shape[2])
                 nc.sync.dma_start(dst, rows[r].bitcast(I32))
 
-        w1 = [keep.tile([P, PASSES, 2 * H], U8, name="w1_%d" % e, align_bytes=64) for e in range(E1)]
+        w1 = {}
 
-        def load_w1(e):
-            nc.sync.dma_start(w1[e][:].bitcast(I32), w1_words[e].rearrange("s p b -> p s b").bitcast(I32))
+        def load_w1(e, first=0, last=PASSES):
+            words = keep.tile([P, last - first, 2 * H], U8, name="w1_%d_%d" % (e, first), align_bytes=64)
+            nc.sync.dma_start(words[:].bitcast(I32), w1_words[e, first:last].rearrange("s p b -> p s b").bitcast(I32))
+            for s in range(first, last):
+                w1[(e, s)] = words[:, s - first, :]
 
-        load_w1(0)
+        load_w1(0, 0, 2)
         load_scales(ws[0], w1_scales[0:3])
         nc.sync.dma_start(gate_rows[0:E1, :], gate1[0].rearrange("(e c) -> e c", e=E1))
 
         picked = keep.tile([P, T], U8, name="picked", align_bytes=64)
         for first in (0, T // 2):
             nc.vector.tensor_copy(picked[:, first : first + T // 2], xs[:].indirect(entries(list1, first, T // 2)))
-        for q in range(4):
+        for q in (0, 2, 1, 3):
             at = LIVE + 64 * (q // 2) + 8 * (q % 2)
             nc.sync.dma_start(xp[QUADRANT * q : QUADRANT * q + LIVE, :, :].bitcast(I32), picked[at : at + 8, :].bitcast(I32))
-        load_w1(1)
+        load_w1(1, 0, 1)
+        load_w1(0, 2, PASSES)
+        load_w1(1, 1, PASSES)
         load_w1(2)
-        load_scales(ws[1], w1_scales[3:6])
-        for e in range(3, 6):
+        load_scales(ws[1], w1_scales[3:5])
+        for e in range(3, 5):
             load_w1(e)
 
         gate_bank = psum.tile([P, P], F32, name="gate_bank", tag="y", bufs=3)
@@ -116,12 +121,24 @@ def tile_moe_ser_none_kernel(
         nc.scalar.copy(gate_cols[:], gate_bank[:, 0:E1])
 
         xg = {}
-        for s, first, count in ((0, 0, 384), (1, 0, 384), (2, 0, 384), (1, 384, 640), (2, 384, 640), (0, 384, 640)):
-            tag = "gate_rows_then_words" if (s, first) == (0, 384) else "xg%d_%d" % (s, first)
+        for s, first, count in ((0, 0, 128), (0, 128, 256), (1, 0, 384), (2, 0, 384), (1, 384, 640), (2, 384, 640), (0, 384, 640)):
+            tag = {(0, 128): "zero_then_words", (0, 384): "gate_rows_then_words"}.get((s, first), "xg%d_%d" % (s, first))
             words = keep.tile([P, count], U32, name="xg%d_%d" % (s, first), tag=tag, align_bytes=64)
             nc.vector.tensor_copy(words[:], x[s].bitcast(U32).indirect(entries(list1, first, count)))
             for j in range(count // C1):
                 xg[(first // C1 + j, s)] = words[:, j * C1 : (j + 1) * C1]
+
+        for turn in range(2):
+            spare = psum.tile([P, H], F32, name="spare", tag="turned")
+            nc.tensor.matmul_mx(
+                out=spare[:],
+                lhsT=xg[(0, 0)].bitcast(FP8X4),
+                lhsT_scale=picked[:, 0:C1],
+                rhs=w1[(0, 0)].bitcast(FP4X4),
+                rhs_scale=picked[:, 0:H],
+                start=True,
+                stop=True,
+            )
 
         c_pairs = [keep.tile([P, T], F32, name="c_pairs%d" % u) for u in range(2)]
         for e in range(E1):
@@ -135,14 +152,14 @@ def tile_moe_ser_none_kernel(
                     out=h[:],
                     lhsT=xg[(e, s)].bitcast(FP8X4),
                     lhsT_scale=xp[:, s - 1, columns] if s else picked[:, columns],
-                    rhs=w1[e][:, s, :].bitcast(FP4X4),
+                    rhs=w1[(e, s)].bitcast(FP4X4),
                     rhs_scale=ws[run % 2][:, plane * H : (plane + 1) * H],
                     start=(s == 0),
                     stop=(s == PASSES - 1),
                 )
             if e == 2:
-                load_scales(ws[0], w1_scales[6:8])
-                for later in range(6, 8):
+                load_scales(ws[0], w1_scales[5:8])
+                for later in range(5, 8):
                     load_w1(later)
             for planes in ((0,), (1,)) if e == 0 else ((0, 1),):
                 count = len(planes)

@@ -26,7 +26,10 @@ QUADRANT = 32
 LIVE = 4
 PER_COLUMN = 16
 RUNS = ((0, 3), (3, 5), (5, 8))
+EARLY = RUNS[0][1] * C1
 PIECES = ((0, 128), (128, 128), (256, 128), (384, 256), (640, 256), (896, 128))
+VECTOR_PIECE = 4
+STORES = 4
 
 
 def tile_moe_ser_none_kernel(
@@ -45,42 +48,49 @@ def tile_moe_ser_none_kernel(
         def entries(list_tile, first, count):
             return list_tile[:, first // PER_COLUMN : (first + count) // PER_COLUMN]
 
+        def moved_rows(quadrant):
+            return LIVE + 2 * QUADRANT * (quadrant // 2) + 2 * LIVE * (quadrant % 2)
+
         xs = keep.tile([P, T], U8, name="xs", align_bytes=64)
         nc.vector.memset(xs[:].bitcast(I32), 0)
         zero = keep.tile([P, 8], I32, name="zero", tag="zero_then_words", align_bytes=64)
         nc.vector.memset(zero[:], 0)
         x_first = keep.tile([P, T], I32, name="x_first")
         nc.sync.dma_start(x_first[:], x_words[0].rearrange("p t d -> p (t d)").bitcast(I32))
-        for q in range(4):
+        for q in range(P // QUADRANT):
             dst = xs[QUADRANT * q : QUADRANT * q + LIVE, :].bitcast(I32)
             nc.scalar.dma_start(dst, x_scales[0, LIVE * q : LIVE * (q + 1), :].bitcast(I32))
-        for half in range(2):
-            at = LIVE + 64 * half
-            src = x_scales[1:3, 8 * half : 8 * half + 8, :].rearrange("s b t -> b s t")
-            nc.sync.dma_start(xs[at : at + 16, :].bitcast(I32), src.bitcast(I32))
+        for q in (0, 2):
+            src = x_scales[1:PASSES, LIVE * q : LIVE * (q + 2), :].rearrange("s b t -> b s t")
+            nc.sync.dma_start(xs[moved_rows(q) : moved_rows(q) + 4 * LIVE, :].bitcast(I32), src.bitcast(I32))
         x_rest = keep.tile([P, PASSES - 1, T], I32, name="x_rest")
         nc.sync.dma_start(x_rest[:], x_words[1:].rearrange("s p t d -> p s (t d)").bitcast(I32))
         x = [x_first[:], x_rest[:, 0, :], x_rest[:, 1, :]]
 
-        slot = PASSES * H
-        ws = [keep.tile([P, (3 - i) * slot], U8, name="ws%d" % i, align_bytes=64) for i in range(2)]
+        ws = []
+        for first, last in RUNS:
+            ws.append(keep.tile([P, (last - first) * PASSES * H], U8, name="ws%d" % first, align_bytes=64))
         nc.vector.memset(ws[0][:].bitcast(I32), 0)
         gate_rows = keep.tile([P, P], F32, name="gate_rows", tag="gate_rows_then_words", align_bytes=64)
         nc.vector.memset(gate_rows[:], 0.0)
         ident = keep.tile([P, P], F32, name="ident")
         nc.vector.memset(ident[:], 0.0)
         make_identity(nc, ident[:], nomemset=True)
-        xp = keep.tile([P, 2, T], U8, name="xp", align_bytes=64)
+        last_zero = keep.tile([P, 8], I32, name="last_zero")
+        nc.vector.memset(last_zero[:], 0)
+        xp = keep.tile([P, PASSES - 1, T], U8, name="xp", align_bytes=64)
         nc.vector.memset(xp[:].bitcast(I32), 0)
 
-        def clear(region):
-            words = region.bitcast(U32)
-            nc.scalar.copy(words, zero[:, 0:1].bitcast(U32).to_broadcast(list(words.shape)))
-
         windows = [keep.tile([P, T], F32, name="window%d" % i) for i in range(2)]
-        clear(ws[1][:])
+
+        def clear_scales(planes, word):
+            words = planes[:].bitcast(U32)
+            nc.scalar.copy(words, word[:, 0:1].bitcast(U32).to_broadcast(list(words.shape)))
+
+        clear_scales(ws[1], zero)
         for window in windows:
             nc.scalar.copy(window[:], zero[:, 0:1].bitcast(F32).to_broadcast([P, T]))
+        clear_scales(ws[2], last_zero)
 
         def load_scales(planes, src):
             rows = src.rearrange("e s (q r) i -> r q (e s) i", r=LIVE)
@@ -97,23 +107,28 @@ def tile_moe_ser_none_kernel(
             for s in range(first, last):
                 w1[(e, s)] = words[:, s - first, :]
 
-        load_w1(0, 0, 2)
-        load_scales(ws[0], w1_scales[0:3])
+        def load_run(run):
+            first, last = RUNS[run]
+            load_scales(ws[run], w1_scales[first:last])
+            for e in range(first, last):
+                load_w1(e)
+
+        load_w1(0, 0, PASSES - 1)
+        load_scales(ws[0], w1_scales[0 : RUNS[0][1]])
         nc.sync.dma_start(gate_rows[0:E1, :], gate1[0].rearrange("(e c) -> e c", e=E1))
 
         picked = keep.tile([P, T], U8, name="picked", align_bytes=64)
         for first in (0, T // 2):
             nc.vector.tensor_copy(picked[:, first : first + T // 2], xs[:].indirect(entries(list1, first, T // 2)))
         for q in (0, 2, 1, 3):
-            at = LIVE + 64 * (q // 2) + 8 * (q % 2)
-            nc.sync.dma_start(xp[QUADRANT * q : QUADRANT * q + LIVE, :, :].bitcast(I32), picked[at : at + 8, :].bitcast(I32))
+            dst = xp[QUADRANT * q : QUADRANT * q + LIVE, :, :].bitcast(I32)
+            nc.sync.dma_start(dst, picked[moved_rows(q) : moved_rows(q) + 2 * LIVE, :].bitcast(I32))
         load_w1(1, 0, 1)
-        load_w1(0, 2, PASSES)
+        load_w1(0, PASSES - 1, PASSES)
         load_w1(1, 1, PASSES)
         load_w1(2)
-        load_scales(ws[1], w1_scales[3:5])
-        for e in range(3, 5):
-            load_w1(e)
+        load_run(1)
+        load_run(2)
 
         gate_bank = psum.tile([P, P], F32, name="gate_bank", tag="y", bufs=3)
         nc.tensor.transpose(gate_bank[:], gate_rows[:], ident[:])
@@ -121,60 +136,50 @@ def tile_moe_ser_none_kernel(
         nc.scalar.copy(gate_cols[:], gate_bank[:, 0:E1])
 
         xg = {}
-        for s, first, count in ((0, 0, 128), (0, 128, 256), (1, 0, 384), (2, 0, 384), (1, 384, 640), (2, 384, 640), (0, 384, 640)):
-            tag = {(0, 128): "zero_then_words", (0, 384): "gate_rows_then_words"}.get((s, first), "xg%d_%d" % (s, first))
-            words = keep.tile([P, count], U32, name="xg%d_%d" % (s, first), tag=tag, align_bytes=64)
+
+        def gather_words(s, first, count, tag):
+            words = keep.tile([P, count], U32, name="xg", tag=tag, align_bytes=64)
             nc.vector.tensor_copy(words[:], x[s].bitcast(U32).indirect(entries(list1, first, count)))
             for j in range(count // C1):
                 xg[(first // C1 + j, s)] = words[:, j * C1 : (j + 1) * C1]
 
-        for turn in range(2):
-            spare = psum.tile([P, H], F32, name="spare", tag="turned")
-            nc.tensor.matmul_mx(
-                out=spare[:],
-                lhsT=xg[(0, 0)].bitcast(FP8X4),
-                lhsT_scale=picked[:, 0:C1],
-                rhs=w1[(0, 0)].bitcast(FP4X4),
-                rhs_scale=picked[:, 0:H],
-                start=True,
-                stop=True,
-            )
+        gather_words(0, 0, C1, "xg_first")
+        gather_words(0, C1, EARLY - C1, "zero_then_words")
+        for first, count in ((0, EARLY), (EARLY, T - EARLY)):
+            for s in range(1, PASSES):
+                gather_words(s, first, count, "xg%d_%d" % (s, first))
+        gather_words(0, EARLY, T - EARLY, "gate_rows_then_words")
 
         c_pairs = [keep.tile([P, T], F32, name="c_pairs%d" % u) for u in range(2)]
         for e in range(E1):
-            run = [i for i in range(len(RUNS)) if RUNS[i][0] <= e < RUNS[i][1]][0]
-            place = e - RUNS[run][0]
+            run = sum(first <= e for first, last in RUNS) - 1
             columns = slice(e * C1, (e + 1) * C1)
             h = psum.tile([P, H], F32, name="h", tag="h", bufs=3)
             for s in range(PASSES):
-                plane = place * PASSES + s
+                plane = (e - RUNS[run][0]) * PASSES + s
                 nc.tensor.matmul_mx(
                     out=h[:],
                     lhsT=xg[(e, s)].bitcast(FP8X4),
                     lhsT_scale=xp[:, s - 1, columns] if s else picked[:, columns],
                     rhs=w1[(e, s)].bitcast(FP4X4),
-                    rhs_scale=ws[run % 2][:, plane * H : (plane + 1) * H],
+                    rhs_scale=ws[run][:, plane * H : (plane + 1) * H],
                     start=(s == 0),
                     stop=(s == PASSES - 1),
                 )
-            if e == 2:
-                load_scales(ws[0], w1_scales[5:8])
-                for later in range(5, 8):
-                    load_w1(later)
-            for planes in ((0,), (1,)) if e == 0 else ((0, 1),):
-                count = len(planes)
-                tag = "gated%d_%d" % (e, planes[0])
-                gated = keep.tile([P, count, P, 2], BF16, name="gated", tag=tag)
-                h_view = h[:].rearrange("c (p u v) -> c u p v", u=2, v=2)
-                nc.scalar.activation(gated[:], h_view[:, planes[0] : planes[-1] + 1], COPY, scale=gate_cols[:, e : e + 1])
-                words = gated[:].rearrange("c u p v -> c (u p v)").bitcast(F32)
+
+            for pairs in ((0,), (1,)) if e == 0 else ((0, 1),):
+                count = len(pairs)
+                gated = keep.tile([P, count, P, 2], BF16, name="gated%d_%d" % (e, pairs[0]))
+                h_pairs = h[:].rearrange("c (p u v) -> c u p v", u=2, v=2)[:, pairs[0] : pairs[-1] + 1]
+                nc.scalar.activation(gated[:], h_pairs, COPY, scale=gate_cols[:, e : e + 1])
+                gated_words = gated[:].rearrange("c u p v -> c (u p v)").bitcast(F32)
                 turned = psum.tile([P, count, C1], F32, name="turned", tag="turned")
                 for j in range(count):
-                    nc.tensor.transpose(turned[:, j, :], words[:, j * P : (j + 1) * P], ident[:])
-                staged = keep.tile([P, count, C1], F32, name="staged%d_%d" % (e, planes[0]))
+                    nc.tensor.transpose(turned[:, j, :], gated_words[:, j * P : (j + 1) * P], ident[:])
+                staged = keep.tile([P, count, C1], F32, name="staged%d_%d" % (e, pairs[0]))
                 nc.scalar.copy(staged[:], turned[:])
-                for j in range(count):
-                    nc.vector.tensor_copy(c_pairs[planes[j]][:].indirect(entries(list1, e * C1, C1)), staged[:, j, :])
+                for j, u in enumerate(pairs):
+                    nc.vector.tensor_copy(c_pairs[u][:].indirect(entries(list1, e * C1, C1)), staged[:, j, :])
 
         nc.sync.dma_start(list2[:], offs2)
         w2 = keep.tile([P, E2, 2 * N], U8, name="w2", align_bytes=64)
@@ -184,31 +189,28 @@ def tile_moe_ser_none_kernel(
         load_scales(ws[1], w2_scales)
 
         products = keep.tile([P, T], F32, name="products")
-        pair_tags = ("pairs0", "pairs1", "pairs0", "scales0", "scales1", "scales0")
-        code_tags = ("codes0", "codes0", "codes0", "codes3", "codes4", "codes3")
-        values, banks = {}, {}
+        woven, banks = {}, {}
 
-        def gather(c):
+        def gather(c, tag):
             first, count = PIECES[c]
-            pairs = keep.tile([P, 2, count], U32, name="pairs%d" % c, tag=pair_tags[c], align_bytes=64)
+            rows = keep.tile([P, 2, count], U32, name="rows%d" % c, tag=tag, align_bytes=64)
             for u in range(2):
-                nc.vector.tensor_copy(pairs[:, u, :], c_pairs[u][:].bitcast(U32).indirect(entries(list2, first, count)))
-            values[c] = keep.tile([P, count, 2], U32, name="values%d" % c, align_bytes=64)
-            nc.scalar.copy(values[c][:], pairs[:].rearrange("p u m -> p m u"))
+                nc.vector.tensor_copy(rows[:, u, :], c_pairs[u][:].bitcast(U32).indirect(entries(list2, first, count)))
+            woven[c] = keep.tile([P, count, 2], U32, name="woven%d" % c, align_bytes=64)
+            nc.scalar.copy(woven[c][:], rows[:].rearrange("p u m -> p m u"))
 
-        def gather_woven(c):
+        def gather_woven(c, tag):
             first, count = PIECES[c]
-            values[c] = keep.tile([P, count, 2], U32, name="values%d" % c, tag=pair_tags[c], align_bytes=64)
+            woven[c] = keep.tile([P, count, 2], U32, name="woven%d" % c, tag=tag, align_bytes=64)
             for u in range(2):
-                nc.vector.tensor_copy(values[c][:, :, u], c_pairs[u][:].bitcast(U32).indirect(entries(list2, first, count)))
+                nc.vector.tensor_copy(woven[c][:, :, u], c_pairs[u][:].bitcast(U32).indirect(entries(list2, first, count)))
 
-        def multiply(c):
+        def multiply(c, tag):
             first, count = PIECES[c]
-            codes = keep.tile([P, count], U32, name="codes%d" % c, tag=code_tags[c], align_bytes=64)
+            codes = keep.tile([P, count], U32, name="codes%d" % c, tag=tag, align_bytes=64)
             scales = keep.tile([P, count], U8, name="scales%d" % c, tag="scales%d" % c, align_bytes=64)
-            nc.vector.quantize_mx(
-                out=codes[:].bitcast(FP8X4), scales=scales[:], in_=values[c][:].rearrange("p m u -> p (m u)").bitcast(BF16)
-            )
+            values = woven[c][:].rearrange("p m u -> p (m u)").bitcast(BF16)
+            nc.vector.quantize_mx(out=codes[:].bitcast(FP8X4), scales=scales[:], in_=values)
             banks[c] = psum.tile([P, count], F32, name="y", tag="y", bufs=3)
             for at in range(0, count, P):
                 f = (first + at) // C2
@@ -224,41 +226,44 @@ def tile_moe_ser_none_kernel(
 
         def gate(c):
             first, count = PIECES[c]
-            nc.vector.tensor_tensor(products[:, first : first + count], banks[c][:], gates[:, first : first + count], MULT)
+            part = slice(first, first + count)
+            nc.vector.tensor_tensor(products[:, part], banks[c][:], gates[:, part], MULT)
 
-        def scatter_scalar(first, count):
-            nc.scalar.activation(windows[0][:].indirect(entries(list2, first, count)), products[:, first : first + count], COPY)
+        def scatter(c):
+            first, count = PIECES[c]
+            offsets, source = entries(list2, first, count), products[:, first : first + count]
+            if c == VECTOR_PIECE:
+                nc.vector.tensor_copy(windows[1][:].indirect(offsets), source)
+            else:
+                nc.scalar.activation(windows[0][:].indirect(offsets), source, COPY)
 
-        def scatter_vector(first, count):
-            nc.vector.tensor_copy(windows[1][:].indirect(entries(list2, first, count)), products[:, first : first + count])
-
-        gather_woven(0)
-        multiply(0)
-        gather(1)
-        gather(2)
+        gather_woven(0, "woven0")
+        multiply(0, "codes0")
+        gather(1, "rows1")
+        gather(2, "woven0")
         gate(0)
-        scatter_scalar(*PIECES[0])
-        multiply(1)
-        gather(3)
+        scatter(0)
+        multiply(1, "codes0")
+        gather(3, "scales0")
         gate(1)
-        scatter_scalar(*PIECES[1])
-        multiply(2)
-        gather(4)
+        scatter(1)
+        multiply(2, "codes0")
+        gather(4, "scales1")
         gate(2)
-        scatter_scalar(*PIECES[2])
-        multiply(3)
-        gather_woven(5)
-        multiply(4)
+        scatter(2)
+        multiply(3, "codes3")
+        gather_woven(5, "scales0")
+        multiply(4, "codes4")
         gate(3)
-        scatter_scalar(*PIECES[3])
-        multiply(5)
+        scatter(3)
+        multiply(5, "codes3")
         gate(4)
         gate(5)
-        scatter_vector(*PIECES[4])
-        scatter_scalar(*PIECES[5])
+        scatter(4)
+        scatter(5)
 
         result = keep.tile([P, T], F32, name="result")
-        for first in range(0, T, T // 4):
-            part = slice(first, first + T // 4)
+        for first in range(0, T, T // STORES):
+            part = slice(first, first + T // STORES)
             nc.vector.tensor_tensor(result[:, part], windows[0][:, part], windows[1][:, part], ADD)
             nc.sync.dma_start(out[:, part], result[:, part])

@@ -76,21 +76,17 @@ def tile_moe_ser_none_kernel(
         ident = keep.tile([P, P], F32, name="ident")
         nc.vector.memset(ident[:], 0.0)
         make_identity(nc, ident[:], nomemset=True)
-        last_zero = keep.tile([P, 8], I32, name="last_zero")
-        nc.vector.memset(last_zero[:], 0)
+        last_zero = keep.tile([P, 8], F32, name="last_zero")
+        nc.vector.memset(last_zero[:], 0.0)
         xp = keep.tile([P, PASSES - 1, T], U8, name="xp", align_bytes=64)
         nc.vector.memset(xp[:].bitcast(I32), 0)
 
         windows = [keep.tile([P, T], F32, name="window%d" % i) for i in range(2)]
-
-        def clear_scales(planes, word):
+        for planes in ws[1:]:
             words = planes[:].bitcast(U32)
-            nc.scalar.copy(words, word[:, 0:1].bitcast(U32).to_broadcast(list(words.shape)))
-
-        clear_scales(ws[1], zero)
-        for window in windows:
-            nc.scalar.copy(window[:], zero[:, 0:1].bitcast(F32).to_broadcast([P, T]))
-        clear_scales(ws[2], last_zero)
+            nc.scalar.copy(words, zero[:, 0:1].bitcast(U32).to_broadcast(list(words.shape)))
+        nc.scalar.copy(windows[0][:], zero[:, 0:1].bitcast(F32).to_broadcast([P, T]))
+        nc.scalar.activation(windows[1][:], last_zero[:, 0:1].to_broadcast([P, T]), COPY)
 
         def load_scales(planes, src):
             rows = src.rearrange("e s (q r) i -> r q (e s) i", r=LIVE)
@@ -114,8 +110,8 @@ def tile_moe_ser_none_kernel(
                 load_w1(e)
 
         load_w1(0, 0, PASSES - 1)
-        load_scales(ws[0], w1_scales[0 : RUNS[0][1]])
         nc.sync.dma_start(gate_rows[0:E1, :], gate1[0].rearrange("(e c) -> e c", e=E1))
+        load_scales(ws[0], w1_scales[0 : RUNS[0][1]])
 
         picked = keep.tile([P, T], U8, name="picked", align_bytes=64)
         for first in (0, T // 2):

from contextlib import ExitStack

import concourse.mybir as mybir
from concourse.masks import make_identity

K, T, H, N = 1536, 1024, 512, 128
E1, C1 = 8, 128
E2, C2 = 4, 256
FLOPS = 2 * T * K * H + 2 * T * H * N

F32 = mybir.dt.float32
BF16 = mybir.dt.bfloat16
I32 = mybir.dt.int32
U32 = mybir.dt.uint32
U16 = mybir.dt.uint16
U8 = mybir.dt.uint8
FP8X4 = mybir.dt.float8_e4m3fn_x4
FP4X4 = mybir.dt.float4_e2m1fn_x4
COPY = mybir.ActivationFunctionType.Copy
MULT = mybir.AluOpType.mult
ADD = mybir.AluOpType.add

P = 128
PASSES = K // 512
QUADRANT = 32
LIVE = 4
PER_COLUMN = 16
RUNS = ((0, 3), (3, 5), (5, 8))
EARLY = RUNS[0][1] * C1
PIECES = ((0, 128), (128, 128), (256, 128), (384, 256), (640, 256), (896, 128))
VECTOR_PIECE = 4
STORES = 4


def tile_moe_ser_none_kernel(
    tc, x_words, x_scales, w1_words, w1_scales, w2_words, w2_scales, gate1, gate2, offs, offs2, out
):
    nc = tc.nc
    with ExitStack() as ctx:
        lists = ctx.enter_context(tc.tile_pool(name="lists", bufs=1))
        keep = ctx.enter_context(tc.tile_pool(name="keep", bufs=1))
        psum = ctx.enter_context(tc.psum_pool(name="psum", bufs=2))

        list1 = lists.tile([P, T // PER_COLUMN], U16, name="list1")
        list2 = lists.tile([P, T // PER_COLUMN], U16, name="list2")
        nc.sync.dma_start(list1[:], offs)

        def entries(list_tile, first, count):
            return list_tile[:, first // PER_COLUMN : (first + count) // PER_COLUMN]

        def moved_rows(quadrant):
            return LIVE + 2 * QUADRANT * (quadrant // 2) + 2 * LIVE * (quadrant % 2)

        xs = keep.tile([P, T], U8, name="xs", align_bytes=64)
        nc.vector.memset(xs[:].bitcast(I32), 0)
        zero = keep.tile([P, 8], I32, name="zero", tag="zero_then_words", align_bytes=64)
        nc.vector.memset(zero[:], 0)
        x_first = keep.tile([P, T], I32, name="x_first")
        nc.sync.dma_start(x_first[:], x_words[0].rearrange("p t d -> p (t d)").bitcast(I32))
        for q in range(P // QUADRANT):
            dst = xs[QUADRANT * q : QUADRANT * q + LIVE, :].bitcast(I32)
            nc.scalar.dma_start(dst, x_scales[0, LIVE * q : LIVE * (q + 1), :].bitcast(I32))
        for q in (0, 2):
            src = x_scales[1:PASSES, LIVE * q : LIVE * (q + 2), :].rearrange("s b t -> b s t")
            nc.sync.dma_start(xs[moved_rows(q) : moved_rows(q) + 4 * LIVE, :].bitcast(I32), src.bitcast(I32))
        x_rest = keep.tile([P, PASSES - 1, T], I32, name="x_rest")
        nc.sync.dma_start(x_rest[:], x_words[1:].rearrange("s p t d -> p s (t d)").bitcast(I32))
        x = [x_first[:], x_rest[:, 0, :], x_rest[:, 1, :]]

        ws = []
        for first, last in RUNS:
            ws.append(keep.tile([P, (last - first) * PASSES * H], U8, name="ws%d" % first, align_bytes=64))
        nc.vector.memset(ws[0][:].bitcast(I32), 0)
        gate_rows = keep.tile([P, P], F32, name="gate_rows", tag="gate_rows_then_words", align_bytes=64)
        nc.vector.memset(gate_rows[:], 0.0)
        ident = keep.tile([P, P], F32, name="ident")
        nc.vector.memset(ident[:], 0.0)
        make_identity(nc, ident[:], nomemset=True)
        last_zero = keep.tile([P, 8], F32, name="last_zero")
        nc.vector.memset(last_zero[:], 0.0)
        xp = keep.tile([P, PASSES - 1, T], U8, name="xp", align_bytes=64)
        nc.vector.memset(xp[:].bitcast(I32), 0)

        windows = [keep.tile([P, T], F32, name="window%d" % i) for i in range(2)]
        for planes in ws[1:]:
            words = planes[:].bitcast(U32)
            nc.scalar.copy(words, zero[:, 0:1].bitcast(U32).to_broadcast(list(words.shape)))
        nc.scalar.copy(windows[0][:], zero[:, 0:1].bitcast(F32).to_broadcast([P, T]))
        nc.scalar.activation(windows[1][:], last_zero[:, 0:1].to_broadcast([P, T]), COPY)

        def load_scales(planes, src):
            rows = src.rearrange("e s (q r) i -> r q (e s) i", r=LIVE)
            width = rows.shape[2] * rows.shape[3]
            for r in range(LIVE):
                dst = planes[r:P:QUADRANT, :width].bitcast(I32).rearrange("q (g i) -> q g i", g=rows.shape[2])
                nc.sync.dma_start(dst, rows[r].bitcast(I32))

        w1 = {}

        def load_w1(e, first=0, last=PASSES):
            words = keep.tile([P, last - first, 2 * H], U8, name="w1_%d_%d" % (e, first), align_bytes=64)
            nc.sync.dma_start(words[:].bitcast(I32), w1_words[e, first:last].rearrange("s p b -> p s b").bitcast(I32))
            for s in range(first, last):
                w1[(e, s)] = words[:, s - first, :]

        def load_run(run):
            first, last = RUNS[run]
            load_scales(ws[run], w1_scales[first:last])
            for e in range(first, last):
                load_w1(e)

        load_w1(0, 0, PASSES - 1)
        nc.sync.dma_start(gate_rows[0:E1, :], gate1[0].rearrange("(e c) -> e c", e=E1))
        load_scales(ws[0], w1_scales[0 : RUNS[0][1]])

        picked = keep.tile([P, T], U8, name="picked", align_bytes=64)
        for first in (0, T // 2):
            nc.vector.tensor_copy(picked[:, first : first + T // 2], xs[:].indirect(entries(list1, first, T // 2)))
        for q in (0, 2, 1, 3):
            dst = xp[QUADRANT * q : QUADRANT * q + LIVE, :, :].bitcast(I32)
            nc.sync.dma_start(dst, picked[moved_rows(q) : moved_rows(q) + 2 * LIVE, :].bitcast(I32))
        load_w1(1, 0, 1)
        load_w1(0, PASSES - 1, PASSES)
        load_w1(1, 1, PASSES)
        load_w1(2)
        load_run(1)
        load_run(2)

        gate_bank = psum.tile([P, P], F32, name="gate_bank", tag="y", bufs=3)
        nc.tensor.transpose(gate_bank[:], gate_rows[:], ident[:])
        gate_cols = keep.tile([P, E1], F32, name="gate_cols")
        nc.scalar.copy(gate_cols[:], gate_bank[:, 0:E1])

        xg = {}

        def gather_words(s, first, count, tag):
            words = keep.tile([P, count], U32, name="xg", tag=tag, align_bytes=64)
            nc.vector.tensor_copy(words[:], x[s].bitcast(U32).indirect(entries(list1, first, count)))
            for j in range(count // C1):
                xg[(first // C1 + j, s)] = words[:, j * C1 : (j + 1) * C1]

        gather_words(0, 0, C1, "xg_first")
        gather_words(0, C1, EARLY - C1, "zero_then_words")
        for first, count in ((0, EARLY), (EARLY, T - EARLY)):
            for s in range(1, PASSES):
                gather_words(s, first, count, "xg%d_%d" % (s, first))
        gather_words(0, EARLY, T - EARLY, "gate_rows_then_words")

        c_pairs = [keep.tile([P, T], F32, name="c_pairs%d" % u) for u in range(2)]
        for e in range(E1):
            run = sum(first <= e for first, last in RUNS) - 1
            columns = slice(e * C1, (e + 1) * C1)
            h = psum.tile([P, H], F32, name="h", tag="h", bufs=3)
            for s in range(PASSES):
                plane = (e - RUNS[run][0]) * PASSES + s
                nc.tensor.matmul_mx(
                    out=h[:],
                    lhsT=xg[(e, s)].bitcast(FP8X4),
                    lhsT_scale=xp[:, s - 1, columns] if s else picked[:, columns],
                    rhs=w1[(e, s)].bitcast(FP4X4),
                    rhs_scale=ws[run][:, plane * H : (plane + 1) * H],
                    start=(s == 0),
                    stop=(s == PASSES - 1),
                )

            for pairs in ((0,), (1,)) if e == 0 else ((0, 1),):
                count = len(pairs)
                gated = keep.tile([P, count, P, 2], BF16, name="gated%d_%d" % (e, pairs[0]))
                h_pairs = h[:].rearrange("c (p u v) -> c u p v", u=2, v=2)[:, pairs[0] : pairs[-1] + 1]
                nc.scalar.activation(gated[:], h_pairs, COPY, scale=gate_cols[:, e : e + 1])
                gated_words = gated[:].rearrange("c u p v -> c (u p v)").bitcast(F32)
                turned = psum.tile([P, count, C1], F32, name="turned", tag="turned")
                for j in range(count):
                    nc.tensor.transpose(turned[:, j, :], gated_words[:, j * P : (j + 1) * P], ident[:])
                staged = keep.tile([P, count, C1], F32, name="staged%d_%d" % (e, pairs[0]))
                nc.scalar.copy(staged[:], turned[:])
                for j, u in enumerate(pairs):
                    nc.vector.tensor_copy(c_pairs[u][:].indirect(entries(list1, e * C1, C1)), staged[:, j, :])

        nc.sync.dma_start(list2[:], offs2)
        w2 = keep.tile([P, E2, 2 * N], U8, name="w2", align_bytes=64)
        nc.sync.dma_start(w2[:].bitcast(I32), w2_words[:, 0].rearrange("f p b -> p f b").bitcast(I32))
        gates = keep.tile([P, T], F32, name="gates")
        nc.sync.dma_start(gates[:], gate2)
        load_scales(ws[1], w2_scales)

        products = keep.tile([P, T], F32, name="products")
        woven, banks = {}, {}

        def gather(c, tag):
            first, count = PIECES[c]
            rows = keep.tile([P, 2, count], U32, name="rows%d" % c, tag=tag, align_bytes=64)
            for u in range(2):
                nc.vector.tensor_copy(rows[:, u, :], c_pairs[u][:].bitcast(U32).indirect(entries(list2, first, count)))
            woven[c] = keep.tile([P, count, 2], U32, name="woven%d" % c, align_bytes=64)
            nc.scalar.copy(woven[c][:], rows[:].rearrange("p u m -> p m u"))

        def gather_woven(c, tag):
            first, count = PIECES[c]
            woven[c] = keep.tile([P, count, 2], U32, name="woven%d" % c, tag=tag, align_bytes=64)
            for u in range(2):
                nc.vector.tensor_copy(woven[c][:, :, u], c_pairs[u][:].bitcast(U32).indirect(entries(list2, first, count)))

        def multiply(c, tag):
            first, count = PIECES[c]
            codes = keep.tile([P, count], U32, name="codes%d" % c, tag=tag, align_bytes=64)
            scales = keep.tile([P, count], U8, name="scales%d" % c, tag="scales%d" % c, align_bytes=64)
            values = woven[c][:].rearrange("p m u -> p (m u)").bitcast(BF16)
            nc.vector.quantize_mx(out=codes[:].bitcast(FP8X4), scales=scales[:], in_=values)
            banks[c] = psum.tile([P, count], F32, name="y", tag="y", bufs=3)
            for at in range(0, count, P):
                f = (first + at) // C2
                nc.tensor.matmul_mx(
                    out=banks[c][:, at : at + P],
                    lhsT=w2[:, f, :].bitcast(FP4X4),
                    lhsT_scale=ws[1][:, f * N : (f + 1) * N],
                    rhs=codes[:, at : at + P].bitcast(FP8X4),
                    rhs_scale=scales[:, at : at + P],
                    start=True,
                    stop=True,
                )

        def gate(c):
            first, count = PIECES[c]
            part = slice(first, first + count)
            nc.vector.tensor_tensor(products[:, part], banks[c][:], gates[:, part], MULT)

        def scatter(c):
            first, count = PIECES[c]
            offsets, source = entries(list2, first, count), products[:, first : first + count]
            if c == VECTOR_PIECE:
                nc.vector.tensor_copy(windows[1][:].indirect(offsets), source)
            else:
                nc.scalar.activation(windows[0][:].indirect(offsets), source, COPY)

        gather_woven(0, "woven0")
        multiply(0, "codes0")
        gather(1, "rows1")
        gather(2, "woven0")
        gate(0)
        scatter(0)
        multiply(1, "codes0")
        gather(3, "scales0")
        gate(1)
        scatter(1)
        multiply(2, "codes0")
        gather(4, "scales1")
        gate(2)
        scatter(2)
        multiply(3, "codes3")
        gather_woven(5, "scales0")
        multiply(4, "codes4")
        gate(3)
        scatter(3)
        multiply(5, "codes3")
        gate(4)
        gate(5)
        scatter(4)
        scatter(5)

        result = keep.tile([P, T], F32, name="result")
        for first in range(0, T, T // STORES):
            part = slice(first, first + T // STORES)
            nc.vector.tensor_tensor(result[:, part], windows[0][:, part], windows[1][:, part], ADD)
            nc.sync.dma_start(out[:, part], result[:, part])
